import numpy as np
import ml_dtypes


def mxq(x, axis, fmt="e4m3"):
    dtype, down = {"e4m3": (ml_dtypes.float8_e4m3fn, 7), "e5m2": (ml_dtypes.float8_e5m2, 14)}[fmt]
    v = np.moveaxis(np.asarray(x, np.float32).astype(ml_dtypes.bfloat16).astype(np.float64), axis, -1)
    blocks = v.reshape(v.shape[:-1] + (-1, 32))
    amax = np.abs(blocks).max(-1, keepdims=True)
    byte = np.maximum(np.where(amax > 0, np.frexp(amax)[1] - 1 + 127, 0) - down, 1)
    scale = np.exp2(byte - 127.0)
    codes = (blocks / scale).astype(np.float32).astype(dtype).astype(np.float64)
    return np.moveaxis((codes * scale).reshape(v.shape), -1, axis)


WIDE = False


def mx_kscale(k):
    if not WIDE:
        return np.ones(k)
    levels = np.array([10, -10, 5, -5, 0])
    if k % 512:
        return np.exp2(np.random.permutation(np.resize(levels, k // 32))).repeat(32)
    a = np.empty((k // 512, 16))
    for p in range(k // 512):
        a[p, :8] = np.random.permutation(np.resize(levels, 8))
        for g in range(8):
            far = levels[np.abs(levels - a[p, g]) >= 10]
            a[p, g + 8] = far[np.random.randint(len(far))]
    return np.exp2(a.ravel()).repeat(32)


def f64(x):
    return np.asarray(x).astype(np.float64)


def striped(idx):
    return np.tile(idx.reshape(-1, 16).T, (8, 1)).astype(np.uint16)


def unstriped(offs):
    return offs[:16].T.reshape(-1).astype(np.int64)


E2M1 = np.array([0.0, 0.5, 1.0, 1.5, 2.0, 3.0, 4.0, 6.0, -0.0, -0.5, -1.0, -1.5, -2.0, -3.0, -4.0, -6.0])


def pack_fp4(w):
    k, n = w.shape
    w = f64(np.asarray(w, np.float32).astype(ml_dtypes.bfloat16)).reshape(k // 32, 32, n)
    amax = np.abs(w).max(1)
    mant, ex = np.frexp(amax / 6.0)
    byte = np.clip(np.where(amax > 0, np.where(mant > 0.5, ex, ex - 1) + 127, 1), 1, 254)
    scaled = (w * np.exp2(127.0 - byte)[:, None, :]).reshape(k, n).astype(np.float32)
    c = np.ascontiguousarray(scaled.reshape(k // 512, 128, 4, n).transpose(0, 1, 3, 2)).astype(ml_dtypes.float4_e2m1fn).view(np.uint8) & 0xF
    words = (c[..., 0::2] | (c[..., 1::2] << 4)).reshape(k // 512, 128, 2 * n)
    return np.ascontiguousarray(words), np.ascontiguousarray(byte.astype(np.uint8).reshape(k // 512, 16, n))


def unpack_fp4(words, scales):
    g, _, n = scales.shape
    words = np.ascontiguousarray(words).reshape(g, 128, n, 2)
    nib = np.empty((g, 128, n, 4), np.uint8)
    nib[..., 0::2] = words & 0xF
    nib[..., 1::2] = words >> 4
    vals = E2M1[nib] * np.repeat(np.exp2(scales.astype(np.float64) - 127.0), 8, axis=1)[..., None]
    return vals.transpose(0, 1, 3, 2).reshape(g * 512, n)


def gelu(v):
    return 0.5 * v * (1.0 + np.tanh(np.sqrt(2.0 / np.pi) * (v + 0.044715 * v**3)))


K, T, S, H, N = 1024, 1024, 512, 512, 128


def setup_inputs():
    n = np.random.standard_normal
    s = mx_kscale(K)[:, None]
    u = mx_kscale(H)
    packed_w1 = pack_fp4(n((K, N)) / np.sqrt(2 * K) / s)
    packed_w3 = pack_fp4(n((H, N)) / np.sqrt(2 * H) / u[:, None])
    return {
        "xT": (n((K, T)) * s).astype(np.float32),
        "w1_words": packed_w1[0],
        "w1_scales": packed_w1[1],
        "w2": (n((K, H)) / np.sqrt(K) / s * u).astype(np.float32),
        "w3_words": packed_w3[0],
        "w3_scales": packed_w3[1],
        "offs": striped(np.random.permutation(T)[:S]),
    }


def reference(xT, w1_words, w1_scales, w2, w3_words, w3_scales, offs):
    xq = mxq(f64(xT)[:, unstriped(offs)], 0, "e4m3")
    h = gelu(mxq(f64(w2), 0, "e4m3").T @ xq)
    return unpack_fp4(w1_words, w1_scales).T @ xq + unpack_fp4(w3_words, w3_scales).T @ mxq(h, 0, "e4m3")

@@ -1,0 +1,237 @@
+from contextlib import ExitStack
+
+import concourse.mybir as mybir
+
+K, T, S, H, N = 1024, 1024, 512, 512, 128
+FLOPS = 2 * S * (K * H + K * N + H * N)
+
+F32 = mybir.dt.float32
+BF16 = mybir.dt.bfloat16
+I32 = mybir.dt.int32
+U32 = mybir.dt.uint32
+U16 = mybir.dt.uint16
+U8 = mybir.dt.uint8
+FP8X4 = mybir.dt.float8_e4m3fn_x4
+FP4X4 = mybir.dt.float4_e2m1fn_x4
+ACT = mybir.ActivationFunctionType
+
+P = 128
+PASSES = K // 512
+CHUNK = 128
+CHUNKS = S // CHUNK
+HALF_T = T // 2
+HALF_H = H // 2
+HALF_M = HALF_H // 4
+
+
+def tile_picked_lora_gelu_e_kernel(
+    tc, xT, w1_words, w1_scales, w2, w3_words, w3_scales, offs, out
+):
+    nc = tc.nc
+    with ExitStack() as ctx:
+        keep = ctx.enter_context(tc.tile_pool(name="keep", bufs=1))
+        psum = ctx.enter_context(tc.psum_pool(name="psum", bufs=1))
+
+        offsets = keep.tile([P, S // 16], U16, name="offsets")
+        zero = keep.tile([P, 1], F32, name="zero")
+        bias = keep.tile([P, 1], F32, name="bias")
+        nc.vector.memset(zero[:], 0.0)
+        nc.scalar.activation(bias[:], zero[:], ACT.Gelu_apprx_tanh)
+
+        w4_scales = keep.tile([P, 3 * N], U8, name="w4_scales", align_bytes=64)
+        nc.vector.memset(w4_scales[:].bitcast(I32), 0)
+        w1_sb = keep.tile([P, PASSES * 2 * N], U8, name="w1_sb", align_bytes=64)
+        w3_sb = keep.tile([P, 2 * N], U8, name="w3_sb", align_bytes=64)
+        for q in range(4):
+            rows = w4_scales[32 * q : 32 * q + 4, :].bitcast(I32)
+            nc.gpsimd.dma_start(
+                out=rows[:, 0 : 2 * N // 4].rearrange("r (z n) -> r z n", z=PASSES),
+                in_=w1_scales[:, 4 * q : 4 * q + 4, :].bitcast(I32).rearrange("z r n -> r z n"),
+            )
+
+        x_raw, w_raw = {}, {}
+        x_rows = xT.rearrange("(z p u e) t -> z u p e t", z=PASSES, u=2, e=2)
+        w_rows = w2.rearrange("(z p j) c -> z p j c", z=PASSES, j=4)
+
+        def load_x(z, u, a):
+            raw = keep.tile([P, 2, HALF_T], F32, name="x_raw_%d_%d_%d" % (z, u, a))
+            nc.sync.dma_start(out=raw[:], in_=x_rows[z, u, :, :, a * HALF_T : (a + 1) * HALF_T])
+            x_raw[z, u, a] = raw
+
+        def load_w(z, a):
+            raw = keep.tile([P, 4, HALF_H], F32, name="w_raw_%d_%d" % (z, a), tag="w_raw_%d_%d" % (z, a), align_bytes=64)
+            nc.sync.dma_start(out=raw[:], in_=w_rows[z, :, :, a * HALF_H : (a + 1) * HALF_H])
+            w_raw[z, a] = raw
+
+        load_x(0, 0, 0)
+        load_x(0, 0, 1)
+        nc.sync.dma_start(offsets[:], offs)
+        load_x(0, 1, 0)
+        load_x(0, 1, 1)
+        load_x(1, 0, 0)
+        load_x(1, 0, 1)
+        load_w(0, 0)
+        load_w(0, 1)
+        nc.sync.dma_start(
+            out=w1_sb[:].bitcast(I32).rearrange("p (z n) -> p z n", z=PASSES),
+            in_=w1_words.bitcast(I32).rearrange("z p n -> p z n"),
+        )
+        load_x(1, 1, 0)
+        load_x(1, 1, 1)
+        load_w(1, 0)
+        load_w(1, 1)
+        nc.sync.dma_start(out=w3_sb[:].bitcast(I32), in_=w3_words[0].bitcast(I32))
+        for q in range(4):
+            rows = w4_scales[32 * q : 32 * q + 4, :].bitcast(I32)
+            nc.sync.dma_start(
+                out=rows[:, 2 * N // 4 : 3 * N // 4],
+                in_=w3_scales[0, 4 * q : 4 * q + 4, :].bitcast(I32),
+            )
+
+        def cast(engine, dst, src):
+            if engine == "vector":
+                nc.vector.tensor_copy(out=dst, in_=src)
+            else:
+                nc.scalar.activation(dst, src, ACT.Copy)
+
+        def cast_pairs(engine, window, z, u, a, c0, c1):
+            t0 = a * HALF_T
+            dst = window[:, 2 * (t0 + c0) : 2 * (t0 + c1)].rearrange("p (t e) -> p t e", e=2)
+            cast(engine, dst, x_raw[z, u, a][:, :, c0:c1].rearrange("p e t -> p t e"))
+
+        def gather(dst, window, n0, n1):
+            nc.vector.tensor_copy(
+                out=dst.bitcast(U32),
+                in_=window[:].bitcast(U32).indirect(offsets[:, n0 // 16 : n1 // 16]),
+            )
+
+        def deal(engine, dst, z, a, t0, t1):
+            cast(engine, dst, w_raw[z, a][:].rearrange("p j (m t) -> p m j t", t=4)[:, :, :, t0:t1])
+
+        windows = {(z, u): keep.tile([P, 2 * T], BF16, name="window_%d_%d" % (z, u)) for z in range(PASSES) for u in range(2)}
+        x_codes = [keep.tile([P, S], U32, name="x_codes_%d" % z, align_bytes=64) for z in range(PASSES)]
+        x_scales = [keep.tile([P, S], U8, name="x_scales_%d" % z, align_bytes=64) for z in range(PASSES)]
+        w_codes = [keep.tile([P, H], U32, name="w_codes_%d" % z, align_bytes=64) for z in range(PASSES)]
+        w_scales = [keep.tile([P, H], U8, name="w_scales_%d" % z, align_bytes=64) for z in range(PASSES)]
+
+        picked0 = keep.tile([P, 2 * S], I32, name="picked_0")
+        for u in range(2):
+            cast_pairs("scalar", windows[0, u], 0, u, 0, 0, HALF_T)
+            cast_pairs("vector", windows[0, u], 0, u, 1, 0, HALF_T)
+            gather(picked0[:, u * S : (u + 1) * S], windows[0, u], 0, S)
+        grouped0 = keep.tile([P, 4 * S], BF16, name="x_grouped_0", align_bytes=64)
+        nc.vector.tensor_copy(
+            out=grouped0[:].bitcast(I32).rearrange("p (n u) -> p n u", u=2),
+            in_=picked0[:].rearrange("p (u n) -> p n u", u=2),
+        )
+        nc.vector.quantize_mx(out=x_codes[0][:].bitcast(FP8X4), scales=x_scales[0][:], in_=grouped0[:])
+
+        HS = S // 2
+        picked1 = [keep.tile([P, 2 * HS], I32, name="picked_1_%d" % b) for b in range(2)]
+        cast_pairs("scalar", windows[1, 0], 1, 0, 0, 0, HALF_T)
+        cast_pairs("scalar", windows[1, 0], 1, 0, 1, 0, HALF_T)
+        for b in range(2):
+            gather(picked1[b][:, 0:HS], windows[1, 0], b * HS, (b + 1) * HS)
+
+        staged0 = keep.tile([P, 4 * H], BF16, name="w_staged_0", align_bytes=64)
+        for a, engine in enumerate(("scalar", "vector")):
+            dst = staged0[:].rearrange("p (t m j) -> p m j t", t=4, j=4)[:, a * HALF_M : (a + 1) * HALF_M]
+            deal(engine, dst, 0, a, 0, 4)
+        nc.vector.quantize_mx(out=w_codes[0][:].bitcast(FP8X4), scales=w_scales[0][:], in_=staged0[:])
+
+        h_banks = [psum.tile([P, 512], F32, name="h_bank_%d" % c) for c in range(CHUNKS)]
+        out_banks = [psum.tile([P, 512], F32, name="out_bank_%d" % c) for c in range(CHUNKS)]
+
+        def hidden_pass(z, c):
+            cols = slice(c * CHUNK, (c + 1) * CHUNK)
+            for t in range(4):
+                nc.tensor.matmul_mx(
+                    out=h_banks[c][:, t * CHUNK : (t + 1) * CHUNK],
+                    lhsT=w_codes[z][:, t * P : (t + 1) * P].bitcast(FP8X4),
+                    lhsT_scale=w_scales[z][:, t * P : (t + 1) * P],
+                    rhs=x_codes[z][:, cols].bitcast(FP8X4),
+                    rhs_scale=x_scales[z][:, cols],
+                    start=(z == 0 and t == 0),
+                    stop=(z == PASSES - 1 and t == 3),
+                )
+
+        def own_pass(z, c):
+            cols = slice(c * CHUNK, (c + 1) * CHUNK)
+            nc.tensor.matmul_mx(
+                out=out_banks[c][:, 0:CHUNK],
+                lhsT=w1_sb[:, z * 2 * N : (z + 1) * 2 * N].bitcast(FP4X4),
+                lhsT_scale=w4_scales[:, z * N : (z + 1) * N],
+                rhs=x_codes[z][:, cols].bitcast(FP8X4),
+                rhs_scale=x_scales[z][:, cols],
+                start=(z == 0),
+                stop=False,
+            )
+
+        for c in range(CHUNKS):
+            hidden_pass(0, c)
+        for c in range(CHUNKS):
+            own_pass(0, c)
+
+        cast_pairs("scalar", windows[1, 1], 1, 1, 0, 0, HALF_T)
+        cast_pairs("vector", windows[1, 1], 1, 1, 1, 0, 352)
+        cast_pairs("scalar", windows[1, 1], 1, 1, 1, 352, HALF_T)
+        for b in range(2):
+            gather(picked1[b][:, HS : 2 * HS], windows[1, 1], b * HS, (b + 1) * HS)
+
+        def quantise_x1(b, grouped):
+            cols = slice(b * HS, (b + 1) * HS)
+            nc.vector.quantize_mx(out=x_codes[1][:, cols].bitcast(FP8X4), scales=x_scales[1][:, cols], in_=grouped[:])
+
+        grouped10 = keep.tile([P, 4 * HS], BF16, name="x_grouped_1_0", align_bytes=64)
+        nc.vector.tensor_copy(
+            out=grouped10[:].bitcast(I32).rearrange("p (n u) -> p n u", u=2),
+            in_=picked1[0][:].rearrange("p (u n) -> p n u", u=2),
+        )
+        quantise_x1(0, grouped10)
+
+        for a, shares in ((0, (("scalar", 0, 4),)), (1, (("vector", 0, 2), ("scalar", 2, 4)))):
+            pieces = []
+            for engine, t0, t1 in shares:
+                staged = keep.tile(
+                    [P, (t1 - t0) * HALF_H], BF16, name="w_staged_1_%d_%d" % (a, t0), align_bytes=64,
+                )
+                deal(engine, staged[:].rearrange("p (t m j) -> p m j t", t=t1 - t0, j=4), 1, a, t0, t1)
+                pieces.extend((t, staged[:, (t - t0) * HALF_H : (t - t0 + 1) * HALF_H]) for t in range(t0, t1))
+            for t, piece in pieces:
+                cols = slice(t * P + a * HALF_M, t * P + (a + 1) * HALF_M)
+                nc.vector.quantize_mx(out=w_codes[1][:, cols].bitcast(FP8X4), scales=w_scales[1][:, cols], in_=piece)
+
+        grouped11 = keep.tile([P, 4 * HS], BF16, name="x_grouped_1_1", tag="w_raw_1_1", align_bytes=64)
+        nc.scalar.copy(
+            out=grouped11[:].bitcast(U32).rearrange("p (n u) -> p n u", u=2),
+            in_=picked1[1][:].bitcast(U32).rearrange("p (u n) -> p n u", u=2),
+        )
+        quantise_x1(1, grouped11)
+
+        for c in range(CHUNKS):
+            hidden_pass(1, c)
+            own_pass(1, c)
+        for c in range(CHUNKS):
+            cols = slice(c * CHUNK, (c + 1) * CHUNK)
+            h = keep.tile([P, 4 * CHUNK], BF16, name="h_%d" % c, align_bytes=64)
+            nc.scalar.activation(
+                h[:].rearrange("p (n t) -> p n t", t=4),
+                h_banks[c][:].rearrange("p (t n) -> p n t", t=4),
+                ACT.Gelu_apprx_tanh,
+                bias=bias[:],
+            )
+            h_codes = keep.tile([P, CHUNK], U32, name="h_codes_%d" % c, align_bytes=64)
+            h_scales = keep.tile([P, CHUNK], U8, name="h_scales_%d" % c, align_bytes=64)
+            nc.vector.quantize_mx(out=h_codes[:].bitcast(FP8X4), scales=h_scales[:], in_=h[:])
+            nc.tensor.matmul_mx(
+                out=out_banks[c][:, 0:CHUNK],
+                lhsT=w3_sb[:].bitcast(FP4X4),
+                lhsT_scale=w4_scales[:, 2 * N : 3 * N],
+                rhs=h_codes[:].bitcast(FP8X4),
+                rhs_scale=h_scales[:],
+                start=False,
+                stop=True,
+            )
+            result = keep.tile([P, CHUNK], F32, name="result_%d" % c)
+            nc.vector.tensor_copy(out=result[:], in_=out_banks[c][:, 0:CHUNK])
+            nc.sync.dma_start(out=out[:, cols], in_=result[:])

@@ -53,33 +53,29 @@ def tile_picked_lora_gelu_e_kernel(
         x_rows = xT.rearrange("(z p u e) t -> z u p e t", z=PASSES, u=2, e=2)
         w_rows = w2.rearrange("(z p j) c -> z p j c", z=PASSES, j=4)
 
-        def load_x(z, u, a):
-            raw = keep.tile([P, 2, HALF_T], F32, name="x_raw_%d_%d_%d" % (z, u, a))
-            nc.sync.dma_start(out=raw[:], in_=x_rows[z, u, :, :, a * HALF_T : (a + 1) * HALF_T])
-            x_raw[z, u, a] = raw
+        def load_x(z, u, t0, t1):
+            raw = keep.tile([P, 2, t1 - t0], F32, name="x_raw_%d_%d_%d" % (z, u, t0))
+            nc.sync.dma_start(out=raw[:], in_=x_rows[z, u, :, :, t0:t1])
+            x_raw[z, u, t0] = raw
 
-        def load_w(z, a):
-            raw = keep.tile([P, 4, HALF_H], F32, name="w_raw_%d_%d" % (z, a), tag="w_raw_%d_%d" % (z, a), align_bytes=64)
-            nc.sync.dma_start(out=raw[:], in_=w_rows[z, :, :, a * HALF_H : (a + 1) * HALF_H])
-            w_raw[z, a] = raw
+        def load_w(z, c0, c1):
+            raw = keep.tile([P, 4, c1 - c0], F32, name="w_raw_%d_%d" % (z, c0), tag="w_raw_%d_%d" % (z, c0), align_bytes=64)
+            nc.sync.dma_start(out=raw[:], in_=w_rows[z, :, :, c0:c1])
+            w_raw[z, c0] = raw
 
-        load_x(0, 0, 0)
-        load_x(0, 0, 1)
+        load_x(0, 0, 0, T)
         nc.sync.dma_start(offsets[:], offs)
-        load_x(0, 1, 0)
-        load_x(0, 1, 1)
-        load_x(1, 0, 0)
-        load_x(1, 0, 1)
-        load_w(0, 0)
-        load_w(0, 1)
+        load_x(0, 1, 0, T)
+        load_x(1, 0, 0, T)
+        load_w(0, 0, H)
+        load_x(1, 1, 0, HALF_T)
+        load_x(1, 1, HALF_T, T)
+        load_w(1, 0, HALF_H)
+        load_w(1, HALF_H, H)
         nc.sync.dma_start(
             out=w1_sb[:].bitcast(I32).rearrange("p (z n) -> p z n", z=PASSES),
             in_=w1_words.bitcast(I32).rearrange("z p n -> p z n"),
         )
-        load_x(1, 1, 0)
-        load_x(1, 1, 1)
-        load_w(1, 0)
-        load_w(1, 1)
         nc.sync.dma_start(out=w3_sb[:].bitcast(I32), in_=w3_words[0].bitcast(I32))
         for q in range(4):
             rows = w4_scales[32 * q : 32 * q + 4, :].bitcast(I32)
@@ -94,10 +90,9 @@ def tile_picked_lora_gelu_e_kernel(
             else:
                 nc.scalar.activation(dst, src, ACT.Copy)
 
-        def cast_pairs(engine, window, z, u, a, c0, c1):
-            t0 = a * HALF_T
-            dst = window[:, 2 * (t0 + c0) : 2 * (t0 + c1)].rearrange("p (t e) -> p t e", e=2)
-            cast(engine, dst, x_raw[z, u, a][:, :, c0:c1].rearrange("p e t -> p t e"))
+        def cast_pairs(engine, z, u, t0, c0, c1):
+            dst = windows[z, u][:, 2 * c0 : 2 * c1].rearrange("p (t e) -> p t e", e=2)
+            cast(engine, dst, x_raw[z, u, t0][:, :, c0 - t0 : c1 - t0].rearrange("p e t -> p t e"))
 
         def gather(dst, window, n0, n1):
             nc.vector.tensor_copy(
@@ -105,8 +100,17 @@ def tile_picked_lora_gelu_e_kernel(
                 in_=window[:].bitcast(U32).indirect(offsets[:, n0 // 16 : n1 // 16]),
             )
 
-        def deal(engine, dst, z, a, t0, t1):
-            cast(engine, dst, w_raw[z, a][:].rearrange("p j (m t) -> p m j t", t=4)[:, :, :, t0:t1])
+        def deal(engine, z, a, c0, m0, t0, t1):
+            staged = keep.tile([P, (t1 - t0) * HALF_H], BF16, name="w_staged_%d_%d_%d" % (z, a, t0), align_bytes=64)
+            dst = staged[:].rearrange("p (t m j) -> p m j t", t=t1 - t0, j=4)
+            src = w_raw[z, c0][:].rearrange("p j (m t) -> p m j t", t=4)
+            cast(engine, dst, src[:, m0 : m0 + HALF_M, :, t0:t1])
+            return [(t, staged[:, (t - t0) * HALF_H : (t - t0 + 1) * HALF_H]) for t in range(t0, t1)]
+
+        def quantise_w(z, a, pieces):
+            for t, piece in pieces:
+                cols = slice(t * P + a * HALF_M, t * P + (a + 1) * HALF_M)
+                nc.vector.quantize_mx(out=w_codes[z][:, cols].bitcast(FP8X4), scales=w_scales[z][:, cols], in_=piece)
 
         windows = {(z, u): keep.tile([P, 2 * T], BF16, name="window_%d_%d" % (z, u)) for z in range(PASSES) for u in range(2)}
         x_codes = [keep.tile([P, S], U32, name="x_codes_%d" % z, align_bytes=64) for z in range(PASSES)]
@@ -114,30 +118,36 @@ def tile_picked_lora_gelu_e_kernel(
         w_codes = [keep.tile([P, H], U32, name="w_codes_%d" % z, align_bytes=64) for z in range(PASSES)]
         w_scales = [keep.tile([P, H], U8, name="w_scales_%d" % z, align_bytes=64) for z in range(PASSES)]
 
-        picked0 = keep.tile([P, 2 * S], I32, name="picked_0")
-        for u in range(2):
-            cast_pairs("scalar", windows[0, u], 0, u, 0, 0, HALF_T)
-            cast_pairs("vector", windows[0, u], 0, u, 1, 0, HALF_T)
-            gather(picked0[:, u * S : (u + 1) * S], windows[0, u], 0, S)
-        grouped0 = keep.tile([P, 4 * S], BF16, name="x_grouped_0", align_bytes=64)
-        nc.vector.tensor_copy(
-            out=grouped0[:].bitcast(I32).rearrange("p (n u) -> p n u", u=2),
-            in_=picked0[:].rearrange("p (u n) -> p n u", u=2),
-        )
-        nc.vector.quantize_mx(out=x_codes[0][:].bitcast(FP8X4), scales=x_scales[0][:], in_=grouped0[:])
-
         HS = S // 2
+        picked0 = [keep.tile([P, 2 * HS], I32, name="picked_0_%d" % b) for b in range(2)]
         picked1 = [keep.tile([P, 2 * HS], I32, name="picked_1_%d" % b) for b in range(2)]
-        cast_pairs("scalar", windows[1, 0], 1, 0, 0, 0, HALF_T)
-        cast_pairs("scalar", windows[1, 0], 1, 0, 1, 0, HALF_T)
+        for u in range(2):
+            cast_pairs("scalar", 0, u, 0, 0, 352)
+            cast_pairs("vector", 0, u, 0, 352, T)
+            for b in range(2):
+                gather(picked0[b][:, u * HS : (u + 1) * HS], windows[0, u], b * HS, (b + 1) * HS)
+        grouped0 = [keep.tile([P, 4 * HS], BF16, name="x_grouped_0_%d" % b, align_bytes=64) for b in range(2)]
+        nc.scalar.copy(
+            out=grouped0[0][:].bitcast(U32).rearrange("p (n u) -> p n u", u=2),
+            in_=picked0[0][:].bitcast(U32).rearrange("p (u n) -> p n u", u=2),
+        )
+        nc.vector.tensor_copy(
+            out=grouped0[1][:].bitcast(I32).rearrange("p (n u) -> p n u", u=2),
+            in_=picked0[1][:].rearrange("p (u n) -> p n u", u=2),
+        )
+        for b in range(2):
+            cols = slice(b * HS, (b + 1) * HS)
+            nc.vector.quantize_mx(out=x_codes[0][:, cols].bitcast(FP8X4), scales=x_scales[0][:, cols], in_=grouped0[b][:])
+
+        cast_pairs("scalar", 1, 0, 0, 0, 640)
+        cast_pairs("vector", 1, 0, 0, 640, T)
         for b in range(2):
             gather(picked1[b][:, 0:HS], windows[1, 0], b * HS, (b + 1) * HS)
 
-        staged0 = keep.tile([P, 4 * H], BF16, name="w_staged_0", align_bytes=64)
-        for a, engine in enumerate(("scalar", "vector")):
-            dst = staged0[:].rearrange("p (t m j) -> p m j t", t=4, j=4)[:, a * HALF_M : (a + 1) * HALF_M]
-            deal(engine, dst, 0, a, 0, 4)
-        nc.vector.quantize_mx(out=w_codes[0][:].bitcast(FP8X4), scales=w_scales[0][:], in_=staged0[:])
+        first = deal("scalar", 0, 0, 0, 0, 0, 4)
+        second = deal("vector", 0, 1, 0, HALF_M, 0, 4)
+        quantise_w(0, 0, first)
+        quantise_w(0, 1, second)
 
         h_banks = [psum.tile([P, 512], F32, name="h_bank_%d" % c) for c in range(CHUNKS)]
         out_banks = [psum.tile([P, 512], F32, name="out_bank_%d" % c) for c in range(CHUNKS)]
@@ -172,9 +182,9 @@ def tile_picked_lora_gelu_e_kernel(
         for c in range(CHUNKS):
             own_pass(0, c)
 
-        cast_pairs("scalar", windows[1, 1], 1, 1, 0, 0, HALF_T)
-        cast_pairs("vector", windows[1, 1], 1, 1, 1, 0, 352)
-        cast_pairs("scalar", windows[1, 1], 1, 1, 1, 352, HALF_T)
+        cast_pairs("scalar", 1, 1, 0, 0, HALF_T)
+        cast_pairs("scalar", 1, 1, HALF_T, HALF_T, HALF_T + 128)
+        cast_pairs("vector", 1, 1, HALF_T, HALF_T + 128, T)
         for b in range(2):
             gather(picked1[b][:, HS : 2 * HS], windows[1, 1], b * HS, (b + 1) * HS)
 
@@ -189,19 +199,10 @@ def tile_picked_lora_gelu_e_kernel(
         )
         quantise_x1(0, grouped10)
 
-        for a, shares in ((0, (("scalar", 0, 4),)), (1, (("vector", 0, 2), ("scalar", 2, 4)))):
-            pieces = []
-            for engine, t0, t1 in shares:
-                staged = keep.tile(
-                    [P, (t1 - t0) * HALF_H], BF16, name="w_staged_1_%d_%d" % (a, t0), align_bytes=64,
-                )
-                deal(engine, staged[:].rearrange("p (t m j) -> p m j t", t=t1 - t0, j=4), 1, a, t0, t1)
-                pieces.extend((t, staged[:, (t - t0) * HALF_H : (t - t0 + 1) * HALF_H]) for t in range(t0, t1))
-            for t, piece in pieces:
-                cols = slice(t * P + a * HALF_M, t * P + (a + 1) * HALF_M)
-                nc.vector.quantize_mx(out=w_codes[1][:, cols].bitcast(FP8X4), scales=w_scales[1][:, cols], in_=piece)
+        quantise_w(1, 0, deal("scalar", 1, 0, 0, 0, 0, 4))
+        quantise_w(1, 1, deal("vector", 1, 1, HALF_H, 0, 0, 2) + deal("scalar", 1, 1, HALF_H, 0, 2, 4))
 
-        grouped11 = keep.tile([P, 4 * HS], BF16, name="x_grouped_1_1", tag="w_raw_1_1", align_bytes=64)
+        grouped11 = keep.tile([P, 4 * HS], BF16, name="x_grouped_1_1", tag="w_raw_1_256", align_bytes=64)
         nc.scalar.copy(
             out=grouped11[:].bitcast(U32).rearrange("p (n u) -> p n u", u=2),
             in_=picked1[1][:].bitcast(U32).rearrange("p (u n) -> p n u", u=2),

@@ -42,19 +42,13 @@ def tile_picked_lora_gelu_e_kernel(
         nc.vector.memset(w4_scales[:].bitcast(I32), 0)
         w1_sb = keep.tile([P, PASSES * 2 * N], U8, name="w1_sb", align_bytes=64)
         w3_sb = keep.tile([P, 2 * N], U8, name="w3_sb", align_bytes=64)
-        for q in range(4):
-            rows = w4_scales[32 * q : 32 * q + 4, :].bitcast(I32)
-            nc.gpsimd.dma_start(
-                out=rows[:, 0 : 2 * N // 4].rearrange("r (z n) -> r z n", z=PASSES),
-                in_=w1_scales[:, 4 * q : 4 * q + 4, :].bitcast(I32).rearrange("z r n -> r z n"),
-            )
 
         x_raw, w_raw = {}, {}
         x_rows = xT.rearrange("(z p u e) t -> z u p e t", z=PASSES, u=2, e=2)
         w_rows = w2.rearrange("(z p j) c -> z p j c", z=PASSES, j=4)
 
         def load_x(z, u, t0, t1):
-            raw = keep.tile([P, 2, t1 - t0], F32, name="x_raw_%d_%d_%d" % (z, u, t0))
+            raw = keep.tile([P, 2, t1 - t0], F32, name="x_raw_%d_%d_%d" % (z, u, t0), tag="x_raw_%d_%d_%d" % (z, u, t0), align_bytes=64)
             nc.sync.dma_start(out=raw[:], in_=x_rows[z, u, :, :, t0:t1])
             x_raw[z, u, t0] = raw
 
@@ -65,17 +59,22 @@ def tile_picked_lora_gelu_e_kernel(
 
         load_x(0, 0, 0, T)
         nc.sync.dma_start(offsets[:], offs)
-        load_x(0, 1, 0, T)
-        load_x(1, 0, 0, T)
-        load_w(0, 0, H)
-        load_x(1, 1, 0, HALF_T)
-        load_x(1, 1, HALF_T, T)
-        load_w(1, 0, HALF_H)
-        load_w(1, HALF_H, H)
+        for z, u in ((0, 1), (1, 0), (1, 1)):
+            load_x(z, u, 0, HALF_T)
+            load_x(z, u, HALF_T, T)
+        for z in range(PASSES):
+            load_w(z, 0, HALF_H)
+            load_w(z, HALF_H, H)
         nc.sync.dma_start(
             out=w1_sb[:].bitcast(I32).rearrange("p (z n) -> p z n", z=PASSES),
             in_=w1_words.bitcast(I32).rearrange("z p n -> p z n"),
         )
+        for q in range(4):
+            rows = w4_scales[32 * q : 32 * q + 4, :].bitcast(I32)
+            nc.sync.dma_start(
+                out=rows[:, 0 : 2 * N // 4].rearrange("r (z n) -> r z n", z=PASSES),
+                in_=w1_scales[:, 4 * q : 4 * q + 4, :].bitcast(I32).rearrange("z r n -> r z n"),
+            )
         nc.sync.dma_start(out=w3_sb[:].bitcast(I32), in_=w3_words[0].bitcast(I32))
         for q in range(4):
             rows = w4_scales[32 * q : 32 * q + 4, :].bitcast(I32)
@@ -100,72 +99,95 @@ def tile_picked_lora_gelu_e_kernel(
                 in_=window[:].bitcast(U32).indirect(offsets[:, n0 // 16 : n1 // 16]),
             )
 
-        def deal(engine, z, a, c0, m0, t0, t1):
-            staged = keep.tile([P, (t1 - t0) * HALF_H], BF16, name="w_staged_%d_%d_%d" % (z, a, t0), align_bytes=64)
+        def deal(engine, z, c0, t0, t1):
+            raw = w_raw[z, c0]
+            staged = keep.tile([P, (t1 - t0) * raw.shape[2]], BF16, name="w_staged_%d_%d_%d" % (z, c0, t0), align_bytes=64)
             dst = staged[:].rearrange("p (t m j) -> p m j t", t=t1 - t0, j=4)
-            src = w_raw[z, c0][:].rearrange("p j (m t) -> p m j t", t=4)
-            cast(engine, dst, src[:, m0 : m0 + HALF_M, :, t0:t1])
-            return [(t, staged[:, (t - t0) * HALF_H : (t - t0 + 1) * HALF_H]) for t in range(t0, t1)]
+            src = raw[:].rearrange("p j (m t) -> p m j t", t=4)
+            cast(engine, dst, src[:, :, :, t0:t1])
+            return staged
 
-        def quantise_w(z, a, pieces):
-            for t, piece in pieces:
-                cols = slice(t * P + a * HALF_M, t * P + (a + 1) * HALF_M)
-                nc.vector.quantize_mx(out=w_codes[z][:, cols].bitcast(FP8X4), scales=w_scales[z][:, cols], in_=piece)
+        def quantise_w(z, first_column, values):
+            cols = slice(first_column, first_column + values.shape[1] // 4)
+            nc.vector.quantize_mx(out=w_codes[z][:, cols].bitcast(FP8X4), scales=w_scales[z][:, cols], in_=values)
 
         windows = {(z, u): keep.tile([P, 2 * T], BF16, name="window_%d_%d" % (z, u)) for z in range(PASSES) for u in range(2)}
-        x_codes = [keep.tile([P, S], U32, name="x_codes_%d" % z, align_bytes=64) for z in range(PASSES)]
+        x_codes = [keep.tile([P, S], U32, name="x_codes_0", align_bytes=64)]
         x_scales = [keep.tile([P, S], U8, name="x_scales_%d" % z, align_bytes=64) for z in range(PASSES)]
         w_codes = [keep.tile([P, H], U32, name="w_codes_%d" % z, align_bytes=64) for z in range(PASSES)]
         w_scales = [keep.tile([P, H], U8, name="w_scales_%d" % z, align_bytes=64) for z in range(PASSES)]
 
         HS = S // 2
-        picked0 = [keep.tile([P, 2 * HS], I32, name="picked_0_%d" % b) for b in range(2)]
-        picked1 = [keep.tile([P, 2 * HS], I32, name="picked_1_%d" % b) for b in range(2)]
-        for u in range(2):
-            cast_pairs("scalar", 0, u, 0, 0, 352)
-            cast_pairs("vector", 0, u, 0, 352, T)
+
+        def weave(engine, z, picked):
+            grouped = keep.tile([P, 4 * S], BF16, name="x_grouped_%d" % z, align_bytes=64)
+            nc.vector.tensor_copy(
+                out=grouped[:].bitcast(I32).rearrange("p (n u) -> p n u", u=2),
+                in_=picked[:].rearrange("p (u n) -> p n u", u=2),
+            )
+            return grouped
+
+        def quantise_x(z, grouped):
+            nc.vector.quantize_mx(out=x_codes[z][:].bitcast(FP8X4), scales=x_scales[z][:], in_=grouped[:])
+
+        picked0 = keep.tile([P, 2 * S], I32, name="picked_0")
+        cast_pairs("scalar", 0, 0, 0, 0, 352)
+        cast_pairs("vector", 0, 0, 0, 352, T)
+        gather(picked0[:, 0:S], windows[0, 0], 0, S)
+        cast_pairs("scalar", 0, 1, 0, 0, HALF_T)
+        cast_pairs("scalar", 0, 1, HALF_T, HALF_T, HALF_T + 160)
+        cast_pairs("vector", 0, 1, HALF_T, HALF_T + 160, T)
+        gather(picked0[:, S : 2 * S], windows[0, 1], 0, S)
+        quantise_x(0, weave("vector", 0, picked0))
+
+        picked1 = keep.tile([P, 2 * S], I32, name="picked_1")
+        cast_pairs("scalar", 1, 0, 0, 0, HALF_T)
+        cast_pairs("scalar", 1, 0, HALF_T, HALF_T, T)
+        gather(picked1[:, 0:S], windows[1, 0], 0, S)
+        cast_pairs("scalar", 1, 1, 0, 0, HALF_T)
+        cast_pairs("scalar", 1, 1, HALF_T, HALF_T, HALF_T + 256)
+        cast_pairs("vector", 1, 1, HALF_T, HALF_T + 256, T)
+        gather(picked1[:, S : 2 * S], windows[1, 1], 0, S)
+        grouped1 = weave("vector", 1, picked1)
+
+        staged0 = [keep.tile([P, 2 * H], BF16, name="w_staged_0_%d" % b, tag="w_staged_0_%d" % b, align_bytes=64) for b in range(2)]
+        for a in range(2):
             for b in range(2):
-                gather(picked0[b][:, u * HS : (u + 1) * HS], windows[0, u], b * HS, (b + 1) * HS)
-        grouped0 = [keep.tile([P, 4 * HS], BF16, name="x_grouped_0_%d" % b, align_bytes=64) for b in range(2)]
-        nc.scalar.copy(
-            out=grouped0[0][:].bitcast(U32).rearrange("p (n u) -> p n u", u=2),
-            in_=picked0[0][:].bitcast(U32).rearrange("p (u n) -> p n u", u=2),
-        )
-        nc.vector.tensor_copy(
-            out=grouped0[1][:].bitcast(I32).rearrange("p (n u) -> p n u", u=2),
-            in_=picked0[1][:].rearrange("p (u n) -> p n u", u=2),
-        )
-        for b in range(2):
-            cols = slice(b * HS, (b + 1) * HS)
-            nc.vector.quantize_mx(out=x_codes[0][:, cols].bitcast(FP8X4), scales=x_scales[0][:, cols], in_=grouped0[b][:])
-
-        cast_pairs("scalar", 1, 0, 0, 0, 640)
-        cast_pairs("vector", 1, 0, 0, 640, T)
-        for b in range(2):
-            gather(picked1[b][:, 0:HS], windows[1, 0], b * HS, (b + 1) * HS)
-
-        first = deal("scalar", 0, 0, 0, 0, 0, 4)
-        second = deal("vector", 0, 1, 0, HALF_M, 0, 4)
-        quantise_w(0, 0, first)
-        quantise_w(0, 1, second)
+                cast(
+                    "scalar",
+                    staged0[b][:].rearrange("p (t m j) -> p m j t", t=2, j=4)[:, a * HALF_M : (a + 1) * HALF_M],
+                    w_raw[0, a * HALF_H][:].rearrange("p j (m t) -> p m j t", t=4)[:, :, :, 2 * b : 2 * b + 2],
+                )
+        quantise_w(0, 0, staged0[0][:])
+        x_codes.append(keep.tile([P, S], U32, name="x_codes_1", tag="w_staged_0_0", align_bytes=64))
+        quantise_x(1, grouped1)
+        quantise_w(0, 2 * P, staged0[1][:])
+        left = deal("scalar", 1, 0, 0, 4)
+        low = deal("vector", 1, HALF_H, 0, 2)
+        high = deal("scalar", 1, HALF_H, 2, 4)
+        for t in range(4):
+            quantise_w(1, t * P, left[:, t * HALF_H : (t + 1) * HALF_H])
+        for t in range(4):
+            staged = low if t < 2 else high
+            quantise_w(1, t * P + HALF_M, staged[:, (t % 2) * HALF_H : (t % 2 + 1) * HALF_H])
 
         h_banks = [psum.tile([P, 512], F32, name="h_bank_%d" % c) for c in range(CHUNKS)]
         out_banks = [psum.tile([P, 512], F32, name="out_bank_%d" % c) for c in range(CHUNKS)]
 
-        def hidden_pass(z, c):
+        def hidden_pass(z, c, opens, ts=range(4)):
             cols = slice(c * CHUNK, (c + 1) * CHUNK)
-            for t in range(4):
+            for t in ts:
                 nc.tensor.matmul_mx(
                     out=h_banks[c][:, t * CHUNK : (t + 1) * CHUNK],
                     lhsT=w_codes[z][:, t * P : (t + 1) * P].bitcast(FP8X4),
                     lhsT_scale=w_scales[z][:, t * P : (t + 1) * P],
                     rhs=x_codes[z][:, cols].bitcast(FP8X4),
                     rhs_scale=x_scales[z][:, cols],
-                    start=(z == 0 and t == 0),
-                    stop=(z == PASSES - 1 and t == 3),
+                    start=(opens and t == 0),
+                    stop=(not opens and t == 3),
                 )
 
-        def own_pass(z, c):
+        def own_pass(z, c, start, stop):
             cols = slice(c * CHUNK, (c + 1) * CHUNK)
             nc.tensor.matmul_mx(
                 out=out_banks[c][:, 0:CHUNK],
@@ -173,48 +195,22 @@ def tile_picked_lora_gelu_e_kernel(
                 lhsT_scale=w4_scales[:, z * N : (z + 1) * N],
                 rhs=x_codes[z][:, cols].bitcast(FP8X4),
                 rhs_scale=x_scales[z][:, cols],
-                start=(z == 0),
-                stop=False,
+                start=start,
+                stop=stop,
             )
 
-        for c in range(CHUNKS):
-            hidden_pass(0, c)
-        for c in range(CHUNKS):
-            own_pass(0, c)
-
-        cast_pairs("scalar", 1, 1, 0, 0, HALF_T)
-        cast_pairs("scalar", 1, 1, HALF_T, HALF_T, HALF_T + 128)
-        cast_pairs("vector", 1, 1, HALF_T, HALF_T + 128, T)
-        for b in range(2):
-            gather(picked1[b][:, HS : 2 * HS], windows[1, 1], b * HS, (b + 1) * HS)
-
-        def quantise_x1(b, grouped):
-            cols = slice(b * HS, (b + 1) * HS)
-            nc.vector.quantize_mx(out=x_codes[1][:, cols].bitcast(FP8X4), scales=x_scales[1][:, cols], in_=grouped[:])
-
-        grouped10 = keep.tile([P, 4 * HS], BF16, name="x_grouped_1_0", align_bytes=64)
-        nc.vector.tensor_copy(
-            out=grouped10[:].bitcast(I32).rearrange("p (n u) -> p n u", u=2),
-            in_=picked1[0][:].rearrange("p (u n) -> p n u", u=2),
-        )
-        quantise_x1(0, grouped10)
-
-        quantise_w(1, 0, deal("scalar", 1, 0, 0, 0, 0, 4))
-        quantise_w(1, 1, deal("vector", 1, 1, HALF_H, 0, 0, 2) + deal("scalar", 1, 1, HALF_H, 0, 2, 4))
-
-        grouped11 = keep.tile([P, 4 * HS], BF16, name="x_grouped_1_1", tag="w_raw_1_256", align_bytes=64)
-        nc.scalar.copy(
-            out=grouped11[:].bitcast(U32).rearrange("p (n u) -> p n u", u=2),
-            in_=picked1[1][:].bitcast(U32).rearrange("p (u n) -> p n u", u=2),
-        )
-        quantise_x1(1, grouped11)
-
-        for c in range(CHUNKS):
-            hidden_pass(1, c)
-            own_pass(1, c)
+        for ts in ((0, 1), (2, 3)):
+            for c in range(CHUNKS - 1):
+                hidden_pass(0, c, True, ts)
+        own_pass(0, CHUNKS - 1, True, False)
+        own_pass(1, CHUNKS - 1, False, False)
+        for c in range(CHUNKS - 1):
+            hidden_pass(1, c, False)
+        hidden_pass(1, CHUNKS - 1, True)
+        hidden_pass(0, CHUNKS - 1, False)
         for c in range(CHUNKS):
             cols = slice(c * CHUNK, (c + 1) * CHUNK)
-            h = keep.tile([P, 4 * CHUNK], BF16, name="h_%d" % c, align_bytes=64)
+            h = keep.tile([P, 4 * CHUNK], BF16, name="h_%d" % c, tag="h_%d" % c, align_bytes=64)
             nc.scalar.activation(
                 h[:].rearrange("p (n t) -> p n t", t=4),
                 h_banks[c][:].rearrange("p (t n) -> p n t", t=4),
@@ -230,9 +226,14 @@ def tile_picked_lora_gelu_e_kernel(
                 lhsT_scale=w4_scales[:, 2 * N : 3 * N],
                 rhs=h_codes[:].bitcast(FP8X4),
                 rhs_scale=h_scales[:],
-                start=False,
-                stop=True,
+                start=(c < CHUNKS - 1),
+                stop=(c == CHUNKS - 1),
             )
-            result = keep.tile([P, CHUNK], F32, name="result_%d" % c)
+            if c < CHUNKS - 1:
+                own_pass(0, c, False, False)
+                own_pass(1, c, False, True)
+        for c in range(CHUNKS):
+            cols = slice(c * CHUNK, (c + 1) * CHUNK)
+            result = keep.tile([P, CHUNK], F32, name="result_%d" % c, tag="h_%d" % (c + 1), align_bytes=64)
             nc.vector.tensor_copy(out=result[:], in_=out_banks[c][:, 0:CHUNK])
             nc.sync.dma_start(out=out[:, cols], in_=result[:])

@@ -19,9 +19,8 @@ P = 128
 PASSES = K // 512
 CHUNK = 128
 CHUNKS = S // CHUNK
-HALF_T = T // 2
 HALF_H = H // 2
-HALF_M = HALF_H // 4
+SCALAR_TOKENS = 352
 
 
 def tile_picked_lora_gelu_e_kernel(
@@ -43,28 +42,18 @@ def tile_picked_lora_gelu_e_kernel(
         w1_sb = keep.tile([P, PASSES * 2 * N], U8, name="w1_sb", align_bytes=64)
         w3_sb = keep.tile([P, 2 * N], U8, name="w3_sb", align_bytes=64)
 
-        x_raw, w_raw = {}, {}
         x_rows = xT.rearrange("(z p u e) t -> z u p e t", z=PASSES, u=2, e=2)
         w_rows = w2.rearrange("(z p j) c -> z p j c", z=PASSES, j=4)
+        x_raw = {(z, u): keep.tile([P, 2, T], F32, name="x_raw_%d_%d" % (z, u), tag="x_raw_%d_%d" % (z, u), align_bytes=64) for z in range(PASSES) for u in range(2)}
+        w_raw = [keep.tile([P, 4, H], F32, name="w_raw_%d" % z, tag="w_raw_%d" % z, align_bytes=64) for z in range(PASSES)]
 
-        def load_x(z, u, t0, t1):
-            raw = keep.tile([P, 2, t1 - t0], F32, name="x_raw_%d_%d_%d" % (z, u, t0), tag="x_raw_%d_%d_%d" % (z, u, t0), align_bytes=64)
-            nc.sync.dma_start(out=raw[:], in_=x_rows[z, u, :, :, t0:t1])
-            x_raw[z, u, t0] = raw
-
-        def load_w(z, c0, c1):
-            raw = keep.tile([P, 4, c1 - c0], F32, name="w_raw_%d_%d" % (z, c0), tag="w_raw_%d_%d" % (z, c0), align_bytes=64)
-            nc.sync.dma_start(out=raw[:], in_=w_rows[z, :, :, c0:c1])
-            w_raw[z, c0] = raw
-
-        load_x(0, 0, 0, T)
+        nc.sync.dma_start(out=x_raw[0, 0][:], in_=x_rows[0, 0])
         nc.sync.dma_start(offsets[:], offs)
-        for z, u in ((0, 1), (1, 0), (1, 1)):
-            load_x(z, u, 0, HALF_T)
-            load_x(z, u, HALF_T, T)
-        for z in range(PASSES):
-            load_w(z, 0, HALF_H)
-            load_w(z, HALF_H, H)
+        nc.sync.dma_start(out=x_raw[0, 1][:], in_=x_rows[0, 1])
+        nc.sync.dma_start(out=x_raw[1, 0][:], in_=x_rows[1, 0])
+        nc.sync.dma_start(out=w_raw[0][:], in_=w_rows[0])
+        nc.sync.dma_start(out=x_raw[1, 1][:], in_=x_rows[1, 1])
+        nc.sync.dma_start(out=w_raw[1][:], in_=w_rows[1])
         nc.sync.dma_start(
             out=w1_sb[:].bitcast(I32).rearrange("p (z n) -> p z n", z=PASSES),
             in_=w1_words.bitcast(I32).rearrange("z p n -> p z n"),
@@ -89,9 +78,12 @@ def tile_picked_lora_gelu_e_kernel(
             else:
                 nc.scalar.activation(dst, src, ACT.Copy)
 
-        def cast_pairs(engine, z, u, t0, c0, c1):
-            dst = windows[z, u][:, 2 * c0 : 2 * c1].rearrange("p (t e) -> p t e", e=2)
-            cast(engine, dst, x_raw[z, u, t0][:, :, c0 - t0 : c1 - t0].rearrange("p e t -> p t e"))
+        windows = {(z, u): keep.tile([P, 2 * T], BF16, name="window_%d_%d" % (z, u)) for z in range(PASSES) for u in range(2)}
+
+        def cast_pairs(z, u, split):
+            for engine, c0, c1 in (("scalar", 0, split), ("vector", split, T)):
+                dst = windows[z, u][:, 2 * c0 : 2 * c1].rearrange("p (t e) -> p t e", e=2)
+                cast(engine, dst, x_raw[z, u][:, :, c0:c1].rearrange("p e t -> p t e"))
 
         def gather(dst, window, n0, n1):
             nc.vector.tensor_copy(
@@ -99,93 +91,99 @@ def tile_picked_lora_gelu_e_kernel(
                 in_=window[:].bitcast(U32).indirect(offsets[:, n0 // 16 : n1 // 16]),
             )
 
-        def deal(engine, z, c0, t0, t1):
-            raw = w_raw[z, c0]
-            staged = keep.tile([P, (t1 - t0) * raw.shape[2]], BF16, name="w_staged_%d_%d_%d" % (z, c0, t0), align_bytes=64)
-            dst = staged[:].rearrange("p (t m j) -> p m j t", t=t1 - t0, j=4)
-            src = raw[:].rearrange("p j (m t) -> p m j t", t=4)
-            cast(engine, dst, src[:, :, :, t0:t1])
-            return staged
+        def weave(engine, dst, picked, n0, n1):
+            src = picked.rearrange("p (u n) -> p n u", u=2)[:, n0:n1]
+            if engine == "vector":
+                nc.vector.tensor_copy(out=dst.bitcast(I32).rearrange("p (n u) -> p n u", u=2), in_=src)
+            else:
+                nc.scalar.copy(dst.bitcast(U32).rearrange("p (n u) -> p n u", u=2), src.bitcast(U32))
 
-        def quantise_w(z, first_column, values):
-            cols = slice(first_column, first_column + values.shape[1] // 4)
-            nc.vector.quantize_mx(out=w_codes[z][:, cols].bitcast(FP8X4), scales=w_scales[z][:, cols], in_=values)
-
-        windows = {(z, u): keep.tile([P, 2 * T], BF16, name="window_%d_%d" % (z, u)) for z in range(PASSES) for u in range(2)}
-        x_codes = [keep.tile([P, S], U32, name="x_codes_0", align_bytes=64)]
+        x_codes = [keep.tile([P, S], U32, name="x_codes_%d" % z, align_bytes=64) for z in range(PASSES)]
         x_scales = [keep.tile([P, S], U8, name="x_scales_%d" % z, align_bytes=64) for z in range(PASSES)]
         w_codes = [keep.tile([P, H], U32, name="w_codes_%d" % z, align_bytes=64) for z in range(PASSES)]
         w_scales = [keep.tile([P, H], U8, name="w_scales_%d" % z, align_bytes=64) for z in range(PASSES)]
+        last_and_staged = keep.tile([P, 2 * CHUNK + 2 * H], BF16, name="last_and_staged", align_bytes=64)
+        staged = {(z, b): keep.tile([P, 2 * H], BF16, name="w_staged_%d_%d" % (z, b), align_bytes=64)[:] for z, b in ((0, 0), (0, 1), (1, 1))}
+        staged[1, 0] = last_and_staged[:, 2 * CHUNK : 2 * CHUNK + 2 * H]
 
-        HS = S // 2
+        def quantise_x(z, n0, n1, values):
+            nc.vector.quantize_mx(out=x_codes[z][:, n0:n1].bitcast(FP8X4), scales=x_scales[z][:, n0:n1], in_=values)
 
-        def weave(engine, z, picked):
-            grouped = keep.tile([P, 4 * S], BF16, name="x_grouped_%d" % z, align_bytes=64)
-            nc.vector.tensor_copy(
-                out=grouped[:].bitcast(I32).rearrange("p (n u) -> p n u", u=2),
-                in_=picked[:].rearrange("p (u n) -> p n u", u=2),
+        def deal(engine, z, b, m0, m1):
+            cast(
+                engine,
+                staged[z, b].rearrange("p (t m j) -> p m j t", t=2, j=4)[:, m0:m1],
+                w_raw[z][:].rearrange("p j (m t) -> p m j t", t=4)[:, m0:m1, :, 2 * b : 2 * b + 2],
             )
-            return grouped
 
-        def quantise_x(z, grouped):
-            nc.vector.quantize_mx(out=x_codes[z][:].bitcast(FP8X4), scales=x_scales[z][:], in_=grouped[:])
+        def quantise_w(z, b):
+            cols = slice(b * HALF_H, (b + 1) * HALF_H)
+            nc.vector.quantize_mx(out=w_codes[z][:, cols].bitcast(FP8X4), scales=w_scales[z][:, cols], in_=staged[z, b])
 
-        picked0 = keep.tile([P, 2 * S], I32, name="picked_0")
-        cast_pairs("scalar", 0, 0, 0, 0, 352)
-        cast_pairs("vector", 0, 0, 0, 352, T)
-        gather(picked0[:, 0:S], windows[0, 0], 0, S)
-        cast_pairs("scalar", 0, 1, 0, 0, HALF_T)
-        cast_pairs("scalar", 0, 1, HALF_T, HALF_T, HALF_T + 160)
-        cast_pairs("vector", 0, 1, HALF_T, HALF_T + 160, T)
-        gather(picked0[:, S : 2 * S], windows[0, 1], 0, S)
-        quantise_x(0, weave("vector", 0, picked0))
-
-        picked1 = keep.tile([P, 2 * S], I32, name="picked_1")
-        cast_pairs("scalar", 1, 0, 0, 0, HALF_T)
-        cast_pairs("scalar", 1, 0, HALF_T, HALF_T, T)
-        gather(picked1[:, 0:S], windows[1, 0], 0, S)
-        cast_pairs("scalar", 1, 1, 0, 0, HALF_T)
-        cast_pairs("scalar", 1, 1, HALF_T, HALF_T, HALF_T + 256)
-        cast_pairs("vector", 1, 1, HALF_T, HALF_T + 256, T)
-        gather(picked1[:, S : 2 * S], windows[1, 1], 0, S)
-        grouped1 = weave("vector", 1, picked1)
-
-        staged0 = [keep.tile([P, 2 * H], BF16, name="w_staged_0_%d" % b, tag="w_staged_0_%d" % b, align_bytes=64) for b in range(2)]
+        HALF_S = S // 2
+        picked0 = [keep.tile([P, S], I32, name="picked_0_%d" % a) for a in range(2)]
+        grouped0 = [keep.tile([P, 2 * S], BF16, name="grouped_0_%d" % a, align_bytes=64) for a in range(2)]
+        for u in range(2):
+            cast_pairs(0, u, SCALAR_TOKENS)
+            for a in range(2):
+                gather(picked0[a][:, u * HALF_S : (u + 1) * HALF_S], windows[0, u], a * HALF_S, (a + 1) * HALF_S)
         for a in range(2):
-            for b in range(2):
-                cast(
-                    "scalar",
-                    staged0[b][:].rearrange("p (t m j) -> p m j t", t=2, j=4)[:, a * HALF_M : (a + 1) * HALF_M],
-                    w_raw[0, a * HALF_H][:].rearrange("p j (m t) -> p m j t", t=4)[:, :, :, 2 * b : 2 * b + 2],
-                )
-        quantise_w(0, 0, staged0[0][:])
-        x_codes.append(keep.tile([P, S], U32, name="x_codes_1", tag="w_staged_0_0", align_bytes=64))
-        quantise_x(1, grouped1)
-        quantise_w(0, 2 * P, staged0[1][:])
-        left = deal("scalar", 1, 0, 0, 4)
-        low = deal("vector", 1, HALF_H, 0, 2)
-        high = deal("scalar", 1, HALF_H, 2, 4)
-        for t in range(4):
-            quantise_w(1, t * P, left[:, t * HALF_H : (t + 1) * HALF_H])
-        for t in range(4):
-            staged = low if t < 2 else high
-            quantise_w(1, t * P + HALF_M, staged[:, (t % 2) * HALF_H : (t % 2 + 1) * HALF_H])
+            weave("vector", grouped0[a][:], picked0[a][:], 0, HALF_S)
+        for a in range(2):
+            quantise_x(0, a * HALF_S, (a + 1) * HALF_S, grouped0[a][:])
+
+        grouped_first = keep.tile([P, 4 * CHUNK], BF16, name="grouped_first", align_bytes=64)
+        picked_mid = keep.tile([P, 4 * CHUNK], I32, name="picked_mid")
+        picked_last = last_and_staged[:, 0 : 4 * CHUNK].bitcast(I32)
+
+        def gather_pass_1(u):
+            nc.vector.tensor_copy(
+                out=grouped_first[:].bitcast(U32).rearrange("p (n u) -> p n u", u=2)[:, :, u],
+                in_=windows[1, u][:].bitcast(U32).indirect(offsets[:, 0 : CHUNK // 16]),
+            )
+            gather(picked_mid[:, u * 2 * CHUNK : (u + 1) * 2 * CHUNK], windows[1, u], CHUNK, 3 * CHUNK)
+
+        cast_pairs(1, 0, 736)
+        gather_pass_1(0)
+        gather(picked_last[:, 0:CHUNK], windows[1, 0], 3 * CHUNK, S)
+        deal("scalar", 0, 0, 0, P)
+        deal("scalar", 0, 1, 0, 32)
+        deal("vector", 0, 1, 32, P)
+        quantise_w(0, 0)
+        quantise_w(0, 1)
+        cast_pairs(1, 1, SCALAR_TOKENS)
+        gather_pass_1(1)
+        quantise_x(1, 0, CHUNK, grouped_first[:])
+
+        for b in range(2):
+            deal("scalar", 1, b, 0, 40)
+            deal("vector", 1, b, 40, P)
+        quantise_w(1, 0)
+        quantise_w(1, 1)
+        grouped_mid = keep.tile([P, 8 * CHUNK], BF16, name="grouped_mid", tag="w_raw_1", align_bytes=64)
+        grouped_last = keep.tile([P, 4 * CHUNK], BF16, name="grouped_last", align_bytes=64)
+        for a in range(2):
+            weave("scalar", grouped_mid[:, a * 4 * CHUNK : (a + 1) * 4 * CHUNK], picked_mid[:], a * CHUNK, (a + 1) * CHUNK)
+        quantise_x(1, CHUNK, 2 * CHUNK, grouped_mid[:, 0 : 4 * CHUNK])
+        gather(picked_last[:, CHUNK : 2 * CHUNK], windows[1, 1], 3 * CHUNK, S)
+        quantise_x(1, 2 * CHUNK, 3 * CHUNK, grouped_mid[:, 4 * CHUNK : 8 * CHUNK])
+        weave("vector", grouped_last[:], picked_last, 0, CHUNK)
+        quantise_x(1, 3 * CHUNK, S, grouped_last[:])
 
         h_banks = [psum.tile([P, 512], F32, name="h_bank_%d" % c) for c in range(CHUNKS)]
         out_banks = [psum.tile([P, 512], F32, name="out_bank_%d" % c) for c in range(CHUNKS)]
 
-        def hidden_pass(z, c, opens, ts=range(4)):
+        def hidden_pass(z, c, t):
             cols = slice(c * CHUNK, (c + 1) * CHUNK)
-            for t in ts:
-                nc.tensor.matmul_mx(
-                    out=h_banks[c][:, t * CHUNK : (t + 1) * CHUNK],
-                    lhsT=w_codes[z][:, t * P : (t + 1) * P].bitcast(FP8X4),
-                    lhsT_scale=w_scales[z][:, t * P : (t + 1) * P],
-                    rhs=x_codes[z][:, cols].bitcast(FP8X4),
-                    rhs_scale=x_scales[z][:, cols],
-                    start=(opens and t == 0),
-                    stop=(not opens and t == 3),
-                )
+            nc.tensor.matmul_mx(
+                out=h_banks[c][:, t * CHUNK : (t + 1) * CHUNK],
+                lhsT=w_codes[z][:, t * P : (t + 1) * P].bitcast(FP8X4),
+                lhsT_scale=w_scales[z][:, t * P : (t + 1) * P],
+                rhs=x_codes[z][:, cols].bitcast(FP8X4),
+                rhs_scale=x_scales[z][:, cols],
+                start=(z == 0 and t == 0),
+                stop=(z == 1 and t == 3),
+            )
 
         def own_pass(z, c, start, stop):
             cols = slice(c * CHUNK, (c + 1) * CHUNK)
@@ -200,14 +198,24 @@ def tile_picked_lora_gelu_e_kernel(
             )
 
         for ts in ((0, 1), (2, 3)):
-            for c in range(CHUNKS - 1):
-                hidden_pass(0, c, True, ts)
+            for c in range(CHUNKS):
+                for t in ts:
+                    hidden_pass(0, c, t)
+        for c in range(2):
+            nc.tensor.matmul_mx(
+                out=out_banks[c][:],
+                lhsT=x_codes[1][:, 0:CHUNK].bitcast(FP8X4),
+                lhsT_scale=x_scales[1][:, 0:CHUNK],
+                rhs=w_codes[0][:].bitcast(FP8X4),
+                rhs_scale=w_scales[0][:],
+                start=True,
+                stop=True,
+            )
+        for c in range(CHUNKS):
+            for t in range(4):
+                hidden_pass(1, c, t)
         own_pass(0, CHUNKS - 1, True, False)
         own_pass(1, CHUNKS - 1, False, False)
-        for c in range(CHUNKS - 1):
-            hidden_pass(1, c, False)
-        hidden_pass(1, CHUNKS - 1, True)
-        hidden_pass(0, CHUNKS - 1, False)
         for c in range(CHUNKS):
             cols = slice(c * CHUNK, (c + 1) * CHUNK)
             h = keep.tile([P, 4 * CHUNK], BF16, name="h_%d" % c, tag="h_%d" % c, align_bytes=64)

@@ -44,16 +44,29 @@ def tile_picked_lora_gelu_e_kernel(
 
         x_rows = xT.rearrange("(z p u e) t -> z u p e t", z=PASSES, u=2, e=2)
         w_rows = w2.rearrange("(z p j) c -> z p j c", z=PASSES, j=4)
-        x_raw = {(z, u): keep.tile([P, 2, T], F32, name="x_raw_%d_%d" % (z, u), tag="x_raw_%d_%d" % (z, u), align_bytes=64) for z in range(PASSES) for u in range(2)}
-        w_raw = [keep.tile([P, 4, H], F32, name="w_raw_%d" % z, tag="w_raw_%d" % z, align_bytes=64) for z in range(PASSES)]
+        x_raw = {(0, u): keep.tile([P, 2 * T], F32, name="x_raw_0_%d" % u, align_bytes=64)[:] for u in range(2)}
+        third = keep.tile([P, 768 + 2 * T], F32, name="third", align_bytes=64)
+        fourth = keep.tile([P, 2 * T + 5 * CHUNK], F32, name="fourth", align_bytes=64)
+        x_raw[1, 0] = third[:, 768 : 768 + 2 * T]
+        x_raw[1, 1] = fourth[:, 0 : 2 * T]
+        x_raw = {key: raw.rearrange("p (e t) -> p e t", e=2) for key, raw in x_raw.items()}
+        last = keep.tile([P, CHUNK + 4 * H], F32, name="last", tag="last", align_bytes=64)
+        w_raw = [keep.tile([P, 4 * H], F32, name="w_raw_0", align_bytes=64)[:], last[:, CHUNK : CHUNK + 4 * H]]
+        w_raw = [raw.rearrange("p (j c) -> p j c", j=4) for raw in w_raw]
 
-        nc.sync.dma_start(out=x_raw[0, 0][:], in_=x_rows[0, 0])
+        nc.sync.dma_start(out=x_raw[0, 0], in_=x_rows[0, 0])
         nc.sync.dma_start(offsets[:], offs)
-        nc.sync.dma_start(out=x_raw[0, 1][:], in_=x_rows[0, 1])
-        nc.sync.dma_start(out=x_raw[1, 0][:], in_=x_rows[1, 0])
-        nc.sync.dma_start(out=w_raw[0][:], in_=w_rows[0])
-        nc.sync.dma_start(out=x_raw[1, 1][:], in_=x_rows[1, 1])
-        nc.sync.dma_start(out=w_raw[1][:], in_=w_rows[1])
+        for q in range(4):
+            rows = w4_scales[32 * q : 32 * q + 4, :].bitcast(I32)
+            nc.sync.dma_start(
+                out=rows[:, 2 * N // 4 : 3 * N // 4],
+                in_=w3_scales[0, 4 * q : 4 * q + 4, :].bitcast(I32),
+            )
+        nc.sync.dma_start(out=x_raw[0, 1], in_=x_rows[0, 1])
+        nc.sync.dma_start(out=x_raw[1, 0], in_=x_rows[1, 0])
+        nc.sync.dma_start(out=w_raw[0], in_=w_rows[0])
+        nc.sync.dma_start(out=x_raw[1, 1], in_=x_rows[1, 1])
+        nc.sync.dma_start(out=w_raw[1], in_=w_rows[1])
         nc.sync.dma_start(
             out=w1_sb[:].bitcast(I32).rearrange("p (z n) -> p z n", z=PASSES),
             in_=w1_words.bitcast(I32).rearrange("z p n -> p z n"),
@@ -65,12 +78,6 @@ def tile_picked_lora_gelu_e_kernel(
                 in_=w1_scales[:, 4 * q : 4 * q + 4, :].bitcast(I32).rearrange("z r n -> r z n"),
             )
         nc.sync.dma_start(out=w3_sb[:].bitcast(I32), in_=w3_words[0].bitcast(I32))
-        for q in range(4):
-            rows = w4_scales[32 * q : 32 * q + 4, :].bitcast(I32)
-            nc.sync.dma_start(
-                out=rows[:, 2 * N // 4 : 3 * N // 4],
-                in_=w3_scales[0, 4 * q : 4 * q + 4, :].bitcast(I32),
-            )
 
         def cast(engine, dst, src):
             if engine == "vector":
@@ -80,10 +87,9 @@ def tile_picked_lora_gelu_e_kernel(
 
         windows = {(z, u): keep.tile([P, 2 * T], BF16, name="window_%d_%d" % (z, u)) for z in range(PASSES) for u in range(2)}
 
-        def cast_pairs(z, u, split):
-            for engine, c0, c1 in (("scalar", 0, split), ("vector", split, T)):
-                dst = windows[z, u][:, 2 * c0 : 2 * c1].rearrange("p (t e) -> p t e", e=2)
-                cast(engine, dst, x_raw[z, u][:, :, c0:c1].rearrange("p e t -> p t e"))
+        def cast_pairs(engine, z, u, c0, c1):
+            dst = windows[z, u][:, 2 * c0 : 2 * c1].rearrange("p (t e) -> p t e", e=2)
+            cast(engine, dst, x_raw[z, u][:, :, c0:c1].rearrange("p e t -> p t e"))
 
         def gather(dst, window, n0, n1):
             nc.vector.tensor_copy(
@@ -102,9 +108,7 @@ def tile_picked_lora_gelu_e_kernel(
         x_scales = [keep.tile([P, S], U8, name="x_scales_%d" % z, align_bytes=64) for z in range(PASSES)]
         w_codes = [keep.tile([P, H], U32, name="w_codes_%d" % z, align_bytes=64) for z in range(PASSES)]
         w_scales = [keep.tile([P, H], U8, name="w_scales_%d" % z, align_bytes=64) for z in range(PASSES)]
-        last_and_staged = keep.tile([P, 2 * CHUNK + 2 * H], BF16, name="last_and_staged", align_bytes=64)
-        staged = {(z, b): keep.tile([P, 2 * H], BF16, name="w_staged_%d_%d" % (z, b), align_bytes=64)[:] for z, b in ((0, 0), (0, 1), (1, 1))}
-        staged[1, 0] = last_and_staged[:, 2 * CHUNK : 2 * CHUNK + 2 * H]
+        staged = {(z, b): keep.tile([P, 2 * H], BF16, name="w_staged_%d_%d" % (z, b), align_bytes=64)[:] for z in range(PASSES) for b in range(2)}
 
         def quantise_x(z, n0, n1, values):
             nc.vector.quantize_mx(out=x_codes[z][:, n0:n1].bitcast(FP8X4), scales=x_scales[z][:, n0:n1], in_=values)
@@ -113,45 +117,48 @@ def tile_picked_lora_gelu_e_kernel(
             cast(
                 engine,
                 staged[z, b].rearrange("p (t m j) -> p m j t", t=2, j=4)[:, m0:m1],
-                w_raw[z][:].rearrange("p j (m t) -> p m j t", t=4)[:, m0:m1, :, 2 * b : 2 * b + 2],
+                w_raw[z].rearrange("p j (m t) -> p m j t", t=4)[:, m0:m1, :, 2 * b : 2 * b + 2],
             )
 
         def quantise_w(z, b):
             cols = slice(b * HALF_H, (b + 1) * HALF_H)
             nc.vector.quantize_mx(out=w_codes[z][:, cols].bitcast(FP8X4), scales=w_scales[z][:, cols], in_=staged[z, b])
 
-        HALF_S = S // 2
-        picked0 = [keep.tile([P, S], I32, name="picked_0_%d" % a) for a in range(2)]
-        grouped0 = [keep.tile([P, 2 * S], BF16, name="grouped_0_%d" % a, align_bytes=64) for a in range(2)]
+        picked0 = keep.tile([P, 2 * S], I32, name="picked_0")
         for u in range(2):
-            cast_pairs(0, u, SCALAR_TOKENS)
-            for a in range(2):
-                gather(picked0[a][:, u * HALF_S : (u + 1) * HALF_S], windows[0, u], a * HALF_S, (a + 1) * HALF_S)
-        for a in range(2):
-            weave("vector", grouped0[a][:], picked0[a][:], 0, HALF_S)
-        for a in range(2):
-            quantise_x(0, a * HALF_S, (a + 1) * HALF_S, grouped0[a][:])
+            cast_pairs("scalar", 0, u, 0, SCALAR_TOKENS)
+            cast_pairs("vector", 0, u, SCALAR_TOKENS, T)
+            gather(picked0[:, u * S : (u + 1) * S], windows[0, u], 0, S)
 
         grouped_first = keep.tile([P, 4 * CHUNK], BF16, name="grouped_first", align_bytes=64)
-        picked_mid = keep.tile([P, 4 * CHUNK], I32, name="picked_mid")
-        picked_last = last_and_staged[:, 0 : 4 * CHUNK].bitcast(I32)
+        grouped_last = fourth[:, 2 * T - CHUNK : 2 * T + CHUNK].bitcast(BF16)
+        picked_mid = fourth[:, 2 * T + CHUNK - 1 : 2 * T + 5 * CHUNK - 1].bitcast(I32)
+
+        def gather_woven(grouped, u, c):
+            nc.vector.tensor_copy(
+                out=grouped.bitcast(U32).rearrange("p (n u) -> p n u", u=2)[:, :, u],
+                in_=windows[1, u][:].bitcast(U32).indirect(offsets[:, c * CHUNK // 16 : (c + 1) * CHUNK // 16]),
+            )
 
         def gather_pass_1(u):
-            nc.vector.tensor_copy(
-                out=grouped_first[:].bitcast(U32).rearrange("p (n u) -> p n u", u=2)[:, :, u],
-                in_=windows[1, u][:].bitcast(U32).indirect(offsets[:, 0 : CHUNK // 16]),
-            )
+            gather_woven(grouped_first[:], u, 0)
             gather(picked_mid[:, u * 2 * CHUNK : (u + 1) * 2 * CHUNK], windows[1, u], CHUNK, 3 * CHUNK)
 
-        cast_pairs(1, 0, 736)
+        cast_pairs("scalar", 1, 0, 0, 272)
+        cast_pairs("vector", 1, 0, 272, T)
         gather_pass_1(0)
-        gather(picked_last[:, 0:CHUNK], windows[1, 0], 3 * CHUNK, S)
+        grouped0 = third[:, 0 : 2 * S].bitcast(BF16)
+        weave("scalar", grouped0, picked0[:], 0, S)
+        quantise_x(0, 0, S, grouped0)
         deal("scalar", 0, 0, 0, P)
         deal("scalar", 0, 1, 0, 32)
         deal("vector", 0, 1, 32, P)
         quantise_w(0, 0)
         quantise_w(0, 1)
-        cast_pairs(1, 1, SCALAR_TOKENS)
+        cast_pairs("scalar", 1, 1, 0, SCALAR_TOKENS)
+        cast_pairs("vector", 1, 1, 704, T)
+        cast_pairs("vector", 1, 1, SCALAR_TOKENS, 704)
+        gather_woven(grouped_last, 0, 3)
         gather_pass_1(1)
         quantise_x(1, 0, CHUNK, grouped_first[:])
 
@@ -160,29 +167,29 @@ def tile_picked_lora_gelu_e_kernel(
             deal("vector", 1, b, 40, P)
         quantise_w(1, 0)
         quantise_w(1, 1)
-        grouped_mid = keep.tile([P, 8 * CHUNK], BF16, name="grouped_mid", tag="w_raw_1", align_bytes=64)
-        grouped_last = keep.tile([P, 4 * CHUNK], BF16, name="grouped_last", align_bytes=64)
-        for a in range(2):
-            weave("scalar", grouped_mid[:, a * 4 * CHUNK : (a + 1) * 4 * CHUNK], picked_mid[:], a * CHUNK, (a + 1) * CHUNK)
-        quantise_x(1, CHUNK, 2 * CHUNK, grouped_mid[:, 0 : 4 * CHUNK])
-        gather(picked_last[:, CHUNK : 2 * CHUNK], windows[1, 1], 3 * CHUNK, S)
-        quantise_x(1, 2 * CHUNK, 3 * CHUNK, grouped_mid[:, 4 * CHUNK : 8 * CHUNK])
-        weave("vector", grouped_last[:], picked_last, 0, CHUNK)
-        quantise_x(1, 3 * CHUNK, S, grouped_last[:])
+        grouped_second = last[:, 0 : 2 * CHUNK].bitcast(BF16)
+        grouped_third = last[:, CHUNK + H - CHUNK : CHUNK + H + CHUNK].bitcast(BF16)
+        weave("scalar", grouped_second, picked_mid, 0, CHUNK)
+        weave("scalar", grouped_third, picked_mid, CHUNK, 2 * CHUNK)
+        quantise_x(1, CHUNK, 2 * CHUNK, grouped_second)
+        gather_woven(grouped_last, 1, 3)
+        quantise_x(1, 2 * CHUNK, 3 * CHUNK, grouped_third)
+        quantise_x(1, 3 * CHUNK, S, grouped_last)
 
+        first_bank = psum.tile([P, 512], F32, name="first_bank", tag="first_bank")
         h_banks = [psum.tile([P, 512], F32, name="h_bank_%d" % c) for c in range(CHUNKS)]
-        out_banks = [psum.tile([P, 512], F32, name="out_bank_%d" % c) for c in range(CHUNKS)]
+        out_banks = {c: psum.tile([P, 512], F32, name="out_bank_%d" % c) for c in range(1, CHUNKS)}
 
         def hidden_pass(z, c, t):
             cols = slice(c * CHUNK, (c + 1) * CHUNK)
             nc.tensor.matmul_mx(
-                out=h_banks[c][:, t * CHUNK : (t + 1) * CHUNK],
+                out=(first_bank if c == 0 and t < 2 else h_banks[c])[:, t * CHUNK : (t + 1) * CHUNK],
                 lhsT=w_codes[z][:, t * P : (t + 1) * P].bitcast(FP8X4),
                 lhsT_scale=w_scales[z][:, t * P : (t + 1) * P],
                 rhs=x_codes[z][:, cols].bitcast(FP8X4),
                 rhs_scale=x_scales[z][:, cols],
-                start=(z == 0 and t == 0),
-                stop=(z == 1 and t == 3),
+                start=(z == 0 and (t == 0 or (c == 0 and t == 2))),
+                stop=(z == 1 and (t == 3 or (c == 0 and t == 1))),
             )
 
         def own_pass(z, c, start, stop):
@@ -201,7 +208,7 @@ def tile_picked_lora_gelu_e_kernel(
             for c in range(CHUNKS):
                 for t in ts:
                     hidden_pass(0, c, t)
-        for c in range(2):
+        for c in (1, 2):
             nc.tensor.matmul_mx(
                 out=out_banks[c][:],
                 lhsT=x_codes[1][:, 0:CHUNK].bitcast(FP8X4),
@@ -219,12 +226,24 @@ def tile_picked_lora_gelu_e_kernel(
         for c in range(CHUNKS):
             cols = slice(c * CHUNK, (c + 1) * CHUNK)
             h = keep.tile([P, 4 * CHUNK], BF16, name="h_%d" % c, tag="h_%d" % c, align_bytes=64)
-            nc.scalar.activation(
-                h[:].rearrange("p (n t) -> p n t", t=4),
-                h_banks[c][:].rearrange("p (t n) -> p n t", t=4),
-                ACT.Gelu_apprx_tanh,
-                bias=bias[:],
-            )
+            if c == 0:
+                pairs = keep.tile([P, 4 * CHUNK], BF16, name="pairs", align_bytes=64)
+                for b, bank in enumerate((first_bank, h_banks[0])):
+                    nc.scalar.activation(
+                        pairs[:, b * 2 * CHUNK : (b + 1) * 2 * CHUNK].rearrange("p (n t) -> p n t", t=2),
+                        bank[:, b * 2 * CHUNK : (b + 1) * 2 * CHUNK].rearrange("p (t n) -> p n t", t=2),
+                        ACT.Gelu_apprx_tanh,
+                        bias=bias[:],
+                    )
+                weave("vector", h[:], pairs[:].bitcast(I32), 0, CHUNK)
+                out_banks[0] = psum.tile([P, 512], F32, name="out_bank_0", tag="first_bank")
+            else:
+                nc.scalar.activation(
+                    h[:].rearrange("p (n t) -> p n t", t=4),
+                    h_banks[c][:].rearrange("p (t n) -> p n t", t=4),
+                    ACT.Gelu_apprx_tanh,
+                    bias=bias[:],
+                )
             h_codes = keep.tile([P, CHUNK], U32, name="h_codes_%d" % c, align_bytes=64)
             h_scales = keep.tile([P, CHUNK], U8, name="h_scales_%d" % c, align_bytes=64)
             nc.vector.quantize_mx(out=h_codes[:].bitcast(FP8X4), scales=h_scales[:], in_=h[:])

@@ -46,9 +46,8 @@ def tile_picked_lora_gelu_e_kernel(
         w_rows = w2.rearrange("(z p j) c -> z p j c", z=PASSES, j=4)
         x_raw = {(0, u): keep.tile([P, 2 * T], F32, name="x_raw_0_%d" % u, align_bytes=64)[:] for u in range(2)}
         third = keep.tile([P, 768 + 2 * T], F32, name="third", align_bytes=64)
-        fourth = keep.tile([P, 2 * T + 5 * CHUNK], F32, name="fourth", align_bytes=64)
         x_raw[1, 0] = third[:, 768 : 768 + 2 * T]
-        x_raw[1, 1] = fourth[:, 0 : 2 * T]
+        x_raw[1, 1] = keep.tile([P, 2 * T], F32, name="x_raw_1_1", align_bytes=64)[:]
         x_raw = {key: raw.rearrange("p (e t) -> p e t", e=2) for key, raw in x_raw.items()}
         last = keep.tile([P, CHUNK + 4 * H], F32, name="last", tag="last", align_bytes=64)
         w_raw = [keep.tile([P, 4 * H], F32, name="w_raw_0", align_bytes=64)[:], last[:, CHUNK : CHUNK + 4 * H]]
@@ -131,8 +130,9 @@ def tile_picked_lora_gelu_e_kernel(
             gather(picked0[:, u * S : (u + 1) * S], windows[0, u], 0, S)
 
         grouped_first = keep.tile([P, 4 * CHUNK], BF16, name="grouped_first", align_bytes=64)
-        grouped_last = fourth[:, 2 * T - CHUNK : 2 * T + CHUNK].bitcast(BF16)
-        picked_mid = fourth[:, 2 * T + CHUNK - 1 : 2 * T + 5 * CHUNK - 1].bitcast(I32)
+        later = keep.tile([P, 6 * CHUNK], I32, name="later", align_bytes=64)
+        grouped_last = later[:, 0 : 2 * CHUNK].bitcast(BF16)
+        picked_mid = later[:, 2 * CHUNK - 1 : 6 * CHUNK - 1]
 
         def gather_woven(grouped, u, c):
             nc.vector.tensor_copy(
@@ -147,6 +147,7 @@ def tile_picked_lora_gelu_e_kernel(
         cast_pairs("scalar", 1, 0, 0, 272)
         cast_pairs("vector", 1, 0, 272, T)
         gather_pass_1(0)
+        gather_woven(grouped_last, 0, 3)
         grouped0 = third[:, 0 : 2 * S].bitcast(BF16)
         weave("scalar", grouped0, picked0[:], 0, S)
         quantise_x(0, 0, S, grouped0)
@@ -156,9 +157,7 @@ def tile_picked_lora_gelu_e_kernel(
         quantise_w(0, 0)
         quantise_w(0, 1)
         cast_pairs("scalar", 1, 1, 0, SCALAR_TOKENS)
-        cast_pairs("vector", 1, 1, 704, T)
-        cast_pairs("vector", 1, 1, SCALAR_TOKENS, 704)
-        gather_woven(grouped_last, 0, 3)
+        cast_pairs("vector", 1, 1, SCALAR_TOKENS, T)
         gather_pass_1(1)
         quantise_x(1, 0, CHUNK, grouped_first[:])
 
@@ -208,13 +207,13 @@ def tile_picked_lora_gelu_e_kernel(
             for c in range(CHUNKS):
                 for t in ts:
                     hidden_pass(0, c, t)
-        for c in (1, 2):
+        for c, width in ((1, 512), (2, 512), (3, 256)):
             nc.tensor.matmul_mx(
-                out=out_banks[c][:],
+                out=out_banks[c][:, 0:width],
                 lhsT=x_codes[1][:, 0:CHUNK].bitcast(FP8X4),
                 lhsT_scale=x_scales[1][:, 0:CHUNK],
-                rhs=w_codes[0][:].bitcast(FP8X4),
-                rhs_scale=w_scales[0][:],
+                rhs=w_codes[0][:, 0:width].bitcast(FP8X4),
+                rhs_scale=w_scales[0][:, 0:width],
                 start=True,
                 stop=True,
             )

@@ -19,8 +19,6 @@ P = 128
 PASSES = K // 512
 CHUNK = 128
 CHUNKS = S // CHUNK
-HALF_H = H // 2
-SCALAR_TOKENS = 352
 
 
 def tile_picked_lora_gelu_e_kernel(
@@ -42,29 +40,34 @@ def tile_picked_lora_gelu_e_kernel(
         w1_sb = keep.tile([P, PASSES * 2 * N], U8, name="w1_sb", align_bytes=64)
         w3_sb = keep.tile([P, 2 * N], U8, name="w3_sb", align_bytes=64)
 
-        x_rows = xT.rearrange("(z p u e) t -> z u p e t", z=PASSES, u=2, e=2)
+        x_rows = xT.rearrange("(z p j) t -> z p j t", z=PASSES, j=4)
         w_rows = w2.rearrange("(z p j) c -> z p j c", z=PASSES, j=4)
-        x_raw = {(0, u): keep.tile([P, 2 * T], F32, name="x_raw_0_%d" % u, align_bytes=64)[:] for u in range(2)}
-        third = keep.tile([P, 768 + 2 * T], F32, name="third", align_bytes=64)
-        x_raw[1, 0] = third[:, 768 : 768 + 2 * T]
-        x_raw[1, 1] = keep.tile([P, 2 * T], F32, name="x_raw_1_1", align_bytes=64)[:]
-        x_raw = {key: raw.rearrange("p (e t) -> p e t", e=2) for key, raw in x_raw.items()}
-        last = keep.tile([P, CHUNK + 4 * H], F32, name="last", tag="last", align_bytes=64)
-        w_raw = [keep.tile([P, 4 * H], F32, name="w_raw_0", align_bytes=64)[:], last[:, CHUNK : CHUNK + 4 * H]]
-        w_raw = [raw.rearrange("p (j c) -> p j c", j=4) for raw in w_raw]
+        x_loads = ((0, 0, 2), (0, 2, 4), (1, 0, 3), (1, 3, 4))
+        x_raw = {(z, j0): keep.tile([P, (j1 - j0) * T], F32, name="x_raw_%d_%d" % (z, j0), align_bytes=64)[:] for z, j0, j1 in x_loads}
+        x_window = {(z, j): x_raw[z, j0][:, (j - j0) * T : (j - j0 + 1) * T] for z, j0, j1 in x_loads for j in range(j0, j1)}
 
-        nc.sync.dma_start(out=x_raw[0, 0], in_=x_rows[0, 0])
+        def load_x(z, j0, j1):
+            nc.sync.dma_start(out=x_raw[z, j0].rearrange("p (j t) -> p j t", t=T), in_=x_rows[z, :, j0:j1])
+
+        turns = ctx.enter_context(tc.tile_pool(name="turns", bufs=1))
+        w_raw = [
+            keep.tile([P, 4 * H], F32, name="w_raw_0", align_bytes=64),
+            turns.tile([P, 4 * H], F32, name="w_raw_1", align_bytes=64, offset=0),
+        ]
+        w_raw = [raw[:].rearrange("p (j c) -> p j c", j=4) for raw in w_raw]
+
+        load_x(*x_loads[0])
         nc.sync.dma_start(offsets[:], offs)
         for q in range(4):
             rows = w4_scales[32 * q : 32 * q + 4, :].bitcast(I32)
             nc.sync.dma_start(
-                out=rows[:, 2 * N // 4 : 3 * N // 4],
-                in_=w3_scales[0, 4 * q : 4 * q + 4, :].bitcast(I32),
+                out=rows[:, 0 : 2 * N // 4].rearrange("r (z n) -> r z n", z=PASSES),
+                in_=w1_scales[:, 4 * q : 4 * q + 4, :].bitcast(I32).rearrange("z r n -> r z n"),
             )
-        nc.sync.dma_start(out=x_raw[0, 1], in_=x_rows[0, 1])
-        nc.sync.dma_start(out=x_raw[1, 0], in_=x_rows[1, 0])
+        load_x(*x_loads[1])
+        load_x(*x_loads[2])
         nc.sync.dma_start(out=w_raw[0], in_=w_rows[0])
-        nc.sync.dma_start(out=x_raw[1, 1], in_=x_rows[1, 1])
+        load_x(*x_loads[3])
         nc.sync.dma_start(out=w_raw[1], in_=w_rows[1])
         nc.sync.dma_start(
             out=w1_sb[:].bitcast(I32).rearrange("p (z n) -> p z n", z=PASSES),
@@ -73,8 +76,8 @@ def tile_picked_lora_gelu_e_kernel(
         for q in range(4):
             rows = w4_scales[32 * q : 32 * q + 4, :].bitcast(I32)
             nc.sync.dma_start(
-                out=rows[:, 0 : 2 * N // 4].rearrange("r (z n) -> r z n", z=PASSES),
-                in_=w1_scales[:, 4 * q : 4 * q + 4, :].bitcast(I32).rearrange("z r n -> r z n"),
+                out=rows[:, 2 * N // 4 : 3 * N // 4],
+                in_=w3_scales[0, 4 * q : 4 * q + 4, :].bitcast(I32),
             )
         nc.sync.dma_start(out=w3_sb[:].bitcast(I32), in_=w3_words[0].bitcast(I32))
 
@@ -84,33 +87,32 @@ def tile_picked_lora_gelu_e_kernel(
             else:
                 nc.scalar.activation(dst, src, ACT.Copy)
 
-        windows = {(z, u): keep.tile([P, 2 * T], BF16, name="window_%d_%d" % (z, u)) for z in range(PASSES) for u in range(2)}
+        planes = [keep.tile([P, 4 * S], F32, name="planes_%d" % z, align_bytes=64) for z in range(PASSES)]
 
-        def cast_pairs(engine, z, u, c0, c1):
-            dst = windows[z, u][:, 2 * c0 : 2 * c1].rearrange("p (t e) -> p t e", e=2)
-            cast(engine, dst, x_raw[z, u][:, :, c0:c1].rearrange("p e t -> p t e"))
+        def gather(engine, z, j, n0, n1):
+            cast(engine, planes[z][:, j * S + n0 : j * S + n1], x_window[z, j].indirect(offsets[:, n0 // 16 : n1 // 16]))
 
-        def gather(dst, window, n0, n1):
-            nc.vector.tensor_copy(
-                out=dst.bitcast(U32),
-                in_=window[:].bitcast(U32).indirect(offsets[:, n0 // 16 : n1 // 16]),
-            )
+        def interleave(engine, dst, z, n0, n1):
+            src = planes[z][:].rearrange("p (j n) -> p j n", j=4)[:, :, n0:n1]
+            cast(engine, dst.rearrange("p (c i j) -> p c j i", i=4, j=4), src.rearrange("p j (c i) -> p c j i", i=4))
 
-        def weave(engine, dst, picked, n0, n1):
-            src = picked.rearrange("p (u n) -> p n u", u=2)[:, n0:n1]
-            if engine == "vector":
-                nc.vector.tensor_copy(out=dst.bitcast(I32).rearrange("p (n u) -> p n u", u=2), in_=src)
-            else:
-                nc.scalar.copy(dst.bitcast(U32).rearrange("p (n u) -> p n u", u=2), src.bitcast(U32))
+        def weave(dst, src):
+            nc.vector.tensor_copy(out=dst.bitcast(I32).rearrange("p (n u) -> p n u", u=2), in_=src.rearrange("p (u n) -> p n u", u=2))
 
         x_codes = [keep.tile([P, S], U32, name="x_codes_%d" % z, align_bytes=64) for z in range(PASSES)]
-        x_scales = [keep.tile([P, S], U8, name="x_scales_%d" % z, align_bytes=64) for z in range(PASSES)]
+        x_scales = [keep.tile([P, width], U8, name="x_scales_%d" % z, align_bytes=64) for z, width in enumerate((S, 2 * CHUNK))]
         w_codes = [keep.tile([P, H], U32, name="w_codes_%d" % z, align_bytes=64) for z in range(PASSES)]
         w_scales = [keep.tile([P, H], U8, name="w_scales_%d" % z, align_bytes=64) for z in range(PASSES)]
+        def x_plane(z, n0, n1):
+            if z == 1 and n0 >= 2 * CHUNK:
+                return late_planes[:, n0 - 2 * CHUNK : n1 - 2 * CHUNK]
+            return x_scales[z][:, n0:n1]
+
         staged = {(z, b): keep.tile([P, 2 * H], BF16, name="w_staged_%d_%d" % (z, b), align_bytes=64)[:] for z in range(PASSES) for b in range(2)}
+        late_planes = turns.tile([P, 2 * CHUNK], U8, name="late_planes", align_bytes=64, offset=0)
 
         def quantise_x(z, n0, n1, values):
-            nc.vector.quantize_mx(out=x_codes[z][:, n0:n1].bitcast(FP8X4), scales=x_scales[z][:, n0:n1], in_=values)
+            nc.vector.quantize_mx(out=x_codes[z][:, n0:n1].bitcast(FP8X4), scales=x_plane(z, n0, n1), in_=values)
 
         def deal(engine, z, b, m0, m1):
             cast(
@@ -119,61 +121,50 @@ def tile_picked_lora_gelu_e_kernel(
                 w_raw[z].rearrange("p j (m t) -> p m j t", t=4)[:, m0:m1, :, 2 * b : 2 * b + 2],
             )
 
-        def quantise_w(z, b):
-            cols = slice(b * HALF_H, (b + 1) * HALF_H)
-            nc.vector.quantize_mx(out=w_codes[z][:, cols].bitcast(FP8X4), scales=w_scales[z][:, cols], in_=staged[z, b])
+        def quantise_w(z, t0, t1):
+            cols = slice(t0 * P, t1 * P)
+            b = t0 // 2
+            values = staged[z, b][:, (t0 - 2 * b) * 4 * P : (t1 - 2 * b) * 4 * P]
+            nc.vector.quantize_mx(out=w_codes[z][:, cols].bitcast(FP8X4), scales=w_scales[z][:, cols], in_=values)
 
-        picked0 = keep.tile([P, 2 * S], I32, name="picked_0")
-        for u in range(2):
-            cast_pairs("scalar", 0, u, 0, SCALAR_TOKENS)
-            cast_pairs("vector", 0, u, SCALAR_TOKENS, T)
-            gather(picked0[:, u * S : (u + 1) * S], windows[0, u], 0, S)
-
-        grouped_first = keep.tile([P, 4 * CHUNK], BF16, name="grouped_first", align_bytes=64)
-        later = keep.tile([P, 6 * CHUNK], I32, name="later", align_bytes=64)
-        grouped_last = later[:, 0 : 2 * CHUNK].bitcast(BF16)
-        picked_mid = later[:, 2 * CHUNK - 1 : 6 * CHUNK - 1]
-
-        def gather_woven(grouped, u, c):
-            nc.vector.tensor_copy(
-                out=grouped.bitcast(U32).rearrange("p (n u) -> p n u", u=2)[:, :, u],
-                in_=windows[1, u][:].bitcast(U32).indirect(offsets[:, c * CHUNK // 16 : (c + 1) * CHUNK // 16]),
-            )
-
-        def gather_pass_1(u):
-            gather_woven(grouped_first[:], u, 0)
-            gather(picked_mid[:, u * 2 * CHUNK : (u + 1) * 2 * CHUNK], windows[1, u], CHUNK, 3 * CHUNK)
-
-        cast_pairs("scalar", 1, 0, 0, 272)
-        cast_pairs("vector", 1, 0, 272, T)
-        gather_pass_1(0)
-        gather_woven(grouped_last, 0, 3)
-        grouped0 = third[:, 0 : 2 * S].bitcast(BF16)
-        weave("scalar", grouped0, picked0[:], 0, S)
-        quantise_x(0, 0, S, grouped0)
-        deal("scalar", 0, 0, 0, P)
-        deal("scalar", 0, 1, 0, 32)
-        deal("vector", 0, 1, 32, P)
-        quantise_w(0, 0)
-        quantise_w(0, 1)
-        cast_pairs("scalar", 1, 1, 0, SCALAR_TOKENS)
-        cast_pairs("vector", 1, 1, SCALAR_TOKENS, T)
-        gather_pass_1(1)
-        quantise_x(1, 0, CHUNK, grouped_first[:])
-
+        grouped0 = [keep.tile([P, 2 * S], BF16, name="grouped_0_%d" % a, align_bytes=64)[:] for a in range(2)]
+        grouped1 = keep.tile([P, 4 * 3 * CHUNK], BF16, name="grouped_1", align_bytes=64)
+        grouped_last = turns.tile([P, 4 * CHUNK], BF16, name="grouped_last", align_bytes=64, offset=1024)
+        gather("scalar", 0, 0, 0, S)
+        gather("vector", 0, 1, 0, S)
+        for a in range(2):
+            gather("scalar", 0, 2, a * 256, (a + 1) * 256)
+            gather("vector", 0, 3, a * 256, (a + 1) * 256)
+        interleave("vector", grouped0[0], 0, 0, 256)
+        interleave("vector", grouped0[1][:, 0:512], 0, 256, 384)
+        interleave("scalar", grouped0[1][:, 512:1024], 0, 384, S)
+        for a in range(2):
+            quantise_x(0, a * 256, (a + 1) * 256, grouped0[a])
+        gather("scalar", 1, 0, 0, S)
+        gather("vector", 1, 1, 0, S)
+        gather("scalar", 1, 2, 0, CHUNK)
+        gather("vector", 1, 2, CHUNK, S)
         for b in range(2):
-            deal("scalar", 1, b, 0, 40)
-            deal("vector", 1, b, 40, P)
-        quantise_w(1, 0)
-        quantise_w(1, 1)
-        grouped_second = last[:, 0 : 2 * CHUNK].bitcast(BF16)
-        grouped_third = last[:, CHUNK + H - CHUNK : CHUNK + H + CHUNK].bitcast(BF16)
-        weave("scalar", grouped_second, picked_mid, 0, CHUNK)
-        weave("scalar", grouped_third, picked_mid, CHUNK, 2 * CHUNK)
-        quantise_x(1, CHUNK, 2 * CHUNK, grouped_second)
-        gather_woven(grouped_last, 1, 3)
-        quantise_x(1, 2 * CHUNK, 3 * CHUNK, grouped_third)
-        quantise_x(1, 3 * CHUNK, S, grouped_last)
+            deal("scalar", 0, b, 0, 48)
+            deal("vector", 0, b, 48, P)
+        quantise_w(0, 0, 2)
+        quantise_w(0, 2, 4)
+        for c in range(CHUNKS):
+            gather("scalar", 1, 3, c * CHUNK, (c + 1) * CHUNK)
+        interleave("vector", grouped1[:, 0:512], 1, 0, 128)
+        interleave("vector", grouped1[:, 512:1024], 1, 128, 256)
+        quantise_x(1, 0, CHUNK, grouped1[:, 0:512])
+        interleave("vector", grouped1[:, 1024:1536], 1, 256, 384)
+        quantise_x(1, CHUNK, 2 * CHUNK, grouped1[:, 512:1024])
+        for b, share in enumerate((44, 48)):
+            deal("scalar", 1, b, 0, share)
+            deal("vector", 1, b, share, P)
+        quantise_w(1, 0, 2)
+        quantise_w(1, 2, 3)
+        quantise_w(1, 3, 4)
+        quantise_x(1, 2 * CHUNK, 3 * CHUNK, grouped1[:, 1024:1536])
+        interleave("vector", grouped_last[:], 1, 384, S)
+        quantise_x(1, 3 * CHUNK, S, grouped_last[:])
 
         first_bank = psum.tile([P, 512], F32, name="first_bank", tag="first_bank")
         h_banks = [psum.tile([P, 512], F32, name="h_bank_%d" % c) for c in range(CHUNKS)]
@@ -186,7 +177,7 @@ def tile_picked_lora_gelu_e_kernel(
                 lhsT=w_codes[z][:, t * P : (t + 1) * P].bitcast(FP8X4),
                 lhsT_scale=w_scales[z][:, t * P : (t + 1) * P],
                 rhs=x_codes[z][:, cols].bitcast(FP8X4),
-                rhs_scale=x_scales[z][:, cols],
+                rhs_scale=x_plane(z, cols.start, cols.stop),
                 start=(z == 0 and (t == 0 or (c == 0 and t == 2))),
                 stop=(z == 1 and (t == 3 or (c == 0 and t == 1))),
             )
@@ -198,7 +189,7 @@ def tile_picked_lora_gelu_e_kernel(
                 lhsT=w1_sb[:, z * 2 * N : (z + 1) * 2 * N].bitcast(FP4X4),
                 lhsT_scale=w4_scales[:, z * N : (z + 1) * N],
                 rhs=x_codes[z][:, cols].bitcast(FP8X4),
-                rhs_scale=x_scales[z][:, cols],
+                rhs_scale=x_plane(z, cols.start, cols.stop),
                 start=start,
                 stop=stop,
             )
@@ -207,21 +198,12 @@ def tile_picked_lora_gelu_e_kernel(
             for c in range(CHUNKS):
                 for t in ts:
                     hidden_pass(0, c, t)
-        for c, width in ((1, 512), (2, 512), (3, 256)):
-            nc.tensor.matmul_mx(
-                out=out_banks[c][:, 0:width],
-                lhsT=x_codes[1][:, 0:CHUNK].bitcast(FP8X4),
-                lhsT_scale=x_scales[1][:, 0:CHUNK],
-                rhs=w_codes[0][:, 0:width].bitcast(FP8X4),
-                rhs_scale=w_scales[0][:, 0:width],
-                start=True,
-                stop=True,
-            )
         for c in range(CHUNKS):
             for t in range(4):
                 hidden_pass(1, c, t)
-        own_pass(0, CHUNKS - 1, True, False)
-        own_pass(1, CHUNKS - 1, False, False)
+        for c in range(1, CHUNKS):
+            own_pass(0, c, True, False)
+            own_pass(1, c, False, False)
         for c in range(CHUNKS):
             cols = slice(c * CHUNK, (c + 1) * CHUNK)
             h = keep.tile([P, 4 * CHUNK], BF16, name="h_%d" % c, tag="h_%d" % c, align_bytes=64)
@@ -234,8 +216,10 @@ def tile_picked_lora_gelu_e_kernel(
                         ACT.Gelu_apprx_tanh,
                         bias=bias[:],
                     )
-                weave("vector", h[:], pairs[:].bitcast(I32), 0, CHUNK)
+                weave(h[:], pairs[:].bitcast(I32))
                 out_banks[0] = psum.tile([P, 512], F32, name="out_bank_0", tag="first_bank")
+                own_pass(0, 0, True, False)
+                own_pass(1, 0, False, False)
             else:
                 nc.scalar.activation(
                     h[:].rearrange("p (n t) -> p n t", t=4),
@@ -252,12 +236,9 @@ def tile_picked_lora_gelu_e_kernel(
                 lhsT_scale=w4_scales[:, 2 * N : 3 * N],
                 rhs=h_codes[:].bitcast(FP8X4),
                 rhs_scale=h_scales[:],
-                start=(c < CHUNKS - 1),
-                stop=(c == CHUNKS - 1),
+                start=False,
+                stop=True,
             )
-            if c < CHUNKS - 1:
-                own_pass(0, c, False, False)
-                own_pass(1, c, False, True)
         for c in range(CHUNKS):
             cols = slice(c * CHUNK, (c + 1) * CHUNK)
             result = keep.tile([P, CHUNK], F32, name="result_%d" % c, tag="h_%d" % (c + 1), align_bytes=64)

@@ -115,11 +115,13 @@ def tile_picked_lora_gelu_e_kernel(
             nc.vector.quantize_mx(out=x_codes[z][:, n0:n1].bitcast(FP8X4), scales=x_plane(z, n0, n1), in_=values)
 
         def deal(engine, z, b, m0, m1):
-            cast(
-                engine,
-                staged[z, b].rearrange("p (t m j) -> p m j t", t=2, j=4)[:, m0:m1],
-                w_raw[z].rearrange("p j (m t) -> p m j t", t=4)[:, m0:m1, :, 2 * b : 2 * b + 2],
-            )
+            if engine == "scalar":
+                dst = staged[z, b].rearrange("p (t m j) -> p m j t", t=2, j=4)[:, m0:m1]
+                src = w_raw[z].rearrange("p j (m t) -> p m j t", t=4)[:, m0:m1, :, 2 * b : 2 * b + 2]
+            else:
+                dst = staged[z, b].rearrange("p (t g i j) -> p g j i t", t=2, i=2, j=4)[:, m0 // 2 : m1 // 2]
+                src = w_raw[z].rearrange("p j (g i t) -> p g j i t", i=2, t=4)[:, m0 // 2 : m1 // 2, :, :, 2 * b : 2 * b + 2]
+            cast(engine, dst, src)
 
         def quantise_w(z, t0, t1):
             cols = slice(t0 * P, t1 * P)

@@ -37,13 +37,13 @@ def tile_picked_lora_gelu_e_kernel(
 
         w4_scales = keep.tile([P, 3 * N], U8, name="w4_scales", align_bytes=64)
         nc.vector.memset(w4_scales[:].bitcast(I32), 0)
-        w1_sb = keep.tile([P, PASSES * 2 * N], U8, name="w1_sb", align_bytes=64)
-        w3_sb = keep.tile([P, 2 * N], U8, name="w3_sb", align_bytes=64)
+        w1_sb = keep.tile([P, PASSES * 2 * N], U8, name="w1_sb", align_bytes=256)
+        w3_sb = keep.tile([P, 2 * N], U8, name="w3_sb", align_bytes=256)
 
         x_rows = xT.rearrange("(z p j) t -> z p j t", z=PASSES, j=4)
         w_rows = w2.rearrange("(z p j) c -> z p j c", z=PASSES, j=4)
         x_loads = ((0, 0, 2), (0, 2, 4), (1, 0, 3), (1, 3, 4))
-        x_raw = {(z, j0): keep.tile([P, (j1 - j0) * T], F32, name="x_raw_%d_%d" % (z, j0), align_bytes=64)[:] for z, j0, j1 in x_loads}
+        x_raw = {(z, j0): keep.tile([P, (j1 - j0) * T], F32, name="x_raw_%d_%d" % (z, j0), align_bytes=256)[:] for z, j0, j1 in x_loads}
         x_window = {(z, j): x_raw[z, j0][:, (j - j0) * T : (j - j0 + 1) * T] for z, j0, j1 in x_loads for j in range(j0, j1)}
 
         def load_x(z, j0, j1):
@@ -51,8 +51,8 @@ def tile_picked_lora_gelu_e_kernel(
 
         turns = ctx.enter_context(tc.tile_pool(name="turns", bufs=1))
         w_raw = [
-            keep.tile([P, 4 * H], F32, name="w_raw_0", align_bytes=64),
-            turns.tile([P, 4 * H], F32, name="w_raw_1", align_bytes=64, offset=0),
+            keep.tile([P, 4 * H], F32, name="w_raw_0", align_bytes=256),
+            turns.tile([P, 4 * H], F32, name="w_raw_1", align_bytes=256, offset=0),
         ]
         w_raw = [raw[:].rearrange("p (j c) -> p j c", j=4) for raw in w_raw]
 
@@ -208,7 +208,7 @@ def tile_picked_lora_gelu_e_kernel(
             own_pass(1, c, False, False)
         for c in range(CHUNKS):
             cols = slice(c * CHUNK, (c + 1) * CHUNK)
-            h = keep.tile([P, 4 * CHUNK], BF16, name="h_%d" % c, tag="h_%d" % c, align_bytes=64)
+            h = keep.tile([P, 4 * CHUNK], BF16, name="h_%d" % c, tag="h_%d" % c, align_bytes=256)
             if c == 0:
                 pairs = keep.tile([P, 4 * CHUNK], BF16, name="pairs", align_bytes=64)
                 for b, bank in enumerate((first_bank, h_banks[0])):
@@ -243,6 +243,6 @@ def tile_picked_lora_gelu_e_kernel(
             )
         for c in range(CHUNKS):
             cols = slice(c * CHUNK, (c + 1) * CHUNK)
-            result = keep.tile([P, CHUNK], F32, name="result_%d" % c, tag="h_%d" % (c + 1), align_bytes=64)
+            result = keep.tile([P, CHUNK], F32, name="result_%d" % c, tag="h_%d" % (c + 1), align_bytes=256)
             nc.vector.tensor_copy(out=result[:], in_=out_banks[c][:, 0:CHUNK])
             nc.sync.dma_start(out=out[:, cols], in_=result[:])

@@ -27,11 +27,12 @@ def tile_picked_lora_gelu_e_kernel(
     nc = tc.nc
     with ExitStack() as ctx:
         keep = ctx.enter_context(tc.tile_pool(name="keep", bufs=1))
+        turns = ctx.enter_context(tc.tile_pool(name="turns", bufs=1))
         psum = ctx.enter_context(tc.psum_pool(name="psum", bufs=1))
 
         offsets = keep.tile([P, S // 16], U16, name="offsets")
-        zero = keep.tile([P, 1], F32, name="zero")
-        bias = keep.tile([P, 1], F32, name="bias")
+        zero = turns.tile([P, 1], F32, name="zero", align_bytes=256, offset=9216)
+        bias = turns.tile([P, 1], F32, name="bias", align_bytes=256, offset=8192)
         nc.vector.memset(zero[:], 0.0)
         nc.scalar.activation(bias[:], zero[:], ACT.Gelu_apprx_tanh)
 
@@ -49,7 +50,6 @@ def tile_picked_lora_gelu_e_kernel(
         def load_x(z, j0, j1):
             nc.sync.dma_start(out=x_raw[z, j0].rearrange("p (j t) -> p j t", t=T), in_=x_rows[z, :, j0:j1])
 
-        turns = ctx.enter_context(tc.tile_pool(name="turns", bufs=1))
         w_raw = [
             keep.tile([P, 4 * H], F32, name="w_raw_0", align_bytes=256),
             turns.tile([P, 4 * H], F32, name="w_raw_1", align_bytes=256, offset=0),
@@ -208,7 +208,7 @@ def tile_picked_lora_gelu_e_kernel(
             own_pass(1, c, False, False)
         for c in range(CHUNKS):
             cols = slice(c * CHUNK, (c + 1) * CHUNK)
-            h = keep.tile([P, 4 * CHUNK], BF16, name="h_%d" % c, tag="h_%d" % c, align_bytes=256)
+            h = keep.tile([P, 4 * CHUNK], BF16, name="h_%d" % c, align_bytes=256)
             if c == 0:
                 pairs = keep.tile([P, 4 * CHUNK], BF16, name="pairs", align_bytes=64)
                 for b, bank in enumerate((first_bank, h_banks[0])):
@@ -227,7 +227,7 @@ def tile_picked_lora_gelu_e_kernel(
                     h[:].rearrange("p (n t) -> p n t", t=4),
                     h_banks[c][:].rearrange("p (t n) -> p n t", t=4),
                     ACT.Gelu_apprx_tanh,
-                    bias=bias[:],
+                    bias=(zero if c == CHUNKS - 1 else bias)[:],
                 )
             h_codes = keep.tile([P, CHUNK], U32, name="h_codes_%d" % c, align_bytes=64)
             h_scales = keep.tile([P, CHUNK], U8, name="h_scales_%d" % c, align_bytes=64)
@@ -241,8 +241,9 @@ def tile_picked_lora_gelu_e_kernel(
                 start=False,
                 stop=True,
             )
+        early = turns.tile([P, 2 * CHUNK], F32, name="early", align_bytes=256, offset=8192)
+        late = turns.tile([P, 2 * CHUNK], F32, name="late", align_bytes=256, offset=9216)
         for c in range(CHUNKS):
-            cols = slice(c * CHUNK, (c + 1) * CHUNK)
-            result = keep.tile([P, CHUNK], F32, name="result_%d" % c, tag="h_%d" % (c + 1), align_bytes=256)
-            nc.vector.tensor_copy(out=result[:], in_=out_banks[c][:, 0:CHUNK])
-            nc.sync.dma_start(out=out[:, cols], in_=result[:])
+            result = (early, late)[c // 2][:, c % 2 * CHUNK : (c % 2 + 1) * CHUNK]
+            nc.vector.tensor_copy(out=result, in_=out_banks[c][:, 0:CHUNK])
+            nc.sync.dma_start(out=out[:, c * CHUNK : (c + 1) * CHUNK], in_=result)

@@ -246,4 +246,7 @@ def tile_picked_lora_gelu_e_kernel(
         for c in range(CHUNKS):
             result = (early, late)[c // 2][:, c % 2 * CHUNK : (c % 2 + 1) * CHUNK]
             nc.vector.tensor_copy(out=result, in_=out_banks[c][:, 0:CHUNK])
-            nc.sync.dma_start(out=out[:, c * CHUNK : (c + 1) * CHUNK], in_=result)
+            if c == 1:
+                nc.sync.dma_start(out=out[:, 0 : 2 * CHUNK], in_=early[:])
+            if c > 1:
+                nc.sync.dma_start(out=out[:, c * CHUNK : (c + 1) * CHUNK], in_=result)

from contextlib import ExitStack

import concourse.mybir as mybir

K, T, S, H, N = 1024, 1024, 512, 512, 128
FLOPS = 2 * S * (K * H + K * N + H * N)

F32 = mybir.dt.float32
BF16 = mybir.dt.bfloat16
I32 = mybir.dt.int32
U32 = mybir.dt.uint32
U16 = mybir.dt.uint16
U8 = mybir.dt.uint8
FP8X4 = mybir.dt.float8_e4m3fn_x4
FP4X4 = mybir.dt.float4_e2m1fn_x4
ACT = mybir.ActivationFunctionType

P = 128
PASSES = K // 512
CHUNK = 128
CHUNKS = S // CHUNK


def tile_picked_lora_gelu_e_kernel(
    tc, xT, w1_words, w1_scales, w2, w3_words, w3_scales, offs, out
):
    nc = tc.nc
    with ExitStack() as ctx:
        keep = ctx.enter_context(tc.tile_pool(name="keep", bufs=1))
        turns = ctx.enter_context(tc.tile_pool(name="turns", bufs=1))
        psum = ctx.enter_context(tc.psum_pool(name="psum", bufs=1))

        offsets = keep.tile([P, S // 16], U16, name="offsets")
        zero = turns.tile([P, 1], F32, name="zero", align_bytes=256, offset=9216)
        bias = turns.tile([P, 1], F32, name="bias", align_bytes=256, offset=8192)
        nc.vector.memset(zero[:], 0.0)
        nc.scalar.activation(bias[:], zero[:], ACT.Gelu_apprx_tanh)

        w4_scales = keep.tile([P, 3 * N], U8, name="w4_scales", align_bytes=64)
        nc.vector.memset(w4_scales[:].bitcast(I32), 0)
        w1_sb = keep.tile([P, PASSES * 2 * N], U8, name="w1_sb", align_bytes=256)
        w3_sb = keep.tile([P, 2 * N], U8, name="w3_sb", align_bytes=256)

        x_rows = xT.rearrange("(z p j) t -> z p j t", z=PASSES, j=4)
        w_rows = w2.rearrange("(z p j) c -> z p j c", z=PASSES, j=4)
        x_loads = ((0, 0, 2), (0, 2, 4), (1, 0, 3), (1, 3, 4))
        x_raw = {(z, j0): keep.tile([P, (j1 - j0) * T], F32, name="x_raw_%d_%d" % (z, j0), align_bytes=256)[:] for z, j0, j1 in x_loads}
        x_window = {(z, j): x_raw[z, j0][:, (j - j0) * T : (j - j0 + 1) * T] for z, j0, j1 in x_loads for j in range(j0, j1)}

        def load_x(z, j0, j1):
            nc.sync.dma_start(out=x_raw[z, j0].rearrange("p (j t) -> p j t", t=T), in_=x_rows[z, :, j0:j1])

        w_raw = [
            keep.tile([P, 4 * H], F32, name="w_raw_0", align_bytes=256),
            turns.tile([P, 4 * H], F32, name="w_raw_1", align_bytes=256, offset=0),
        ]
        w_raw = [raw[:].rearrange("p (j c) -> p j c", j=4) for raw in w_raw]

        load_x(*x_loads[0])
        nc.sync.dma_start(offsets[:], offs)
        for q in range(4):
            rows = w4_scales[32 * q : 32 * q + 4, :].bitcast(I32)
            nc.sync.dma_start(
                out=rows[:, 0 : 2 * N // 4].rearrange("r (z n) -> r z n", z=PASSES),
                in_=w1_scales[:, 4 * q : 4 * q + 4, :].bitcast(I32).rearrange("z r n -> r z n"),
            )
        load_x(*x_loads[1])
        load_x(*x_loads[2])
        nc.sync.dma_start(out=w_raw[0], in_=w_rows[0])
        load_x(*x_loads[3])
        nc.sync.dma_start(out=w_raw[1], in_=w_rows[1])
        nc.sync.dma_start(
            out=w1_sb[:].bitcast(I32).rearrange("p (z n) -> p z n", z=PASSES),
            in_=w1_words.bitcast(I32).rearrange("z p n -> p z n"),
        )
        for q in range(4):
            rows = w4_scales[32 * q : 32 * q + 4, :].bitcast(I32)
            nc.sync.dma_start(
                out=rows[:, 2 * N // 4 : 3 * N // 4],
                in_=w3_scales[0, 4 * q : 4 * q + 4, :].bitcast(I32),
            )
        nc.sync.dma_start(out=w3_sb[:].bitcast(I32), in_=w3_words[0].bitcast(I32))

        def cast(engine, dst, src):
            if engine == "vector":
                nc.vector.tensor_copy(out=dst, in_=src)
            else:
                nc.scalar.activation(dst, src, ACT.Copy)

        planes = [keep.tile([P, 4 * S], F32, name="planes_%d" % z, align_bytes=64) for z in range(PASSES)]

        def gather(engine, z, j, n0, n1):
            cast(engine, planes[z][:, j * S + n0 : j * S + n1], x_window[z, j].indirect(offsets[:, n0 // 16 : n1 // 16]))

        def interleave(engine, dst, z, n0, n1):
            src = planes[z][:].rearrange("p (j n) -> p j n", j=4)[:, :, n0:n1]
            cast(engine, dst.rearrange("p (c i j) -> p c j i", i=4, j=4), src.rearrange("p j (c i) -> p c j i", i=4))

        def weave(dst, src):
            nc.vector.tensor_copy(out=dst.bitcast(I32).rearrange("p (n u) -> p n u", u=2), in_=src.rearrange("p (u n) -> p n u", u=2))

        x_codes = [keep.tile([P, S], U32, name="x_codes_%d" % z, align_bytes=64) for z in range(PASSES)]
        x_scales = [keep.tile([P, width], U8, name="x_scales_%d" % z, align_bytes=64) for z, width in enumerate((S, 2 * CHUNK))]
        w_codes = [keep.tile([P, H], U32, name="w_codes_%d" % z, align_bytes=64) for z in range(PASSES)]
        w_scales = [keep.tile([P, H], U8, name="w_scales_%d" % z, align_bytes=64) for z in range(PASSES)]
        def x_plane(z, n0, n1):
            if z == 1 and n0 >= 2 * CHUNK:
                return late_planes[:, n0 - 2 * CHUNK : n1 - 2 * CHUNK]
            return x_scales[z][:, n0:n1]

        staged = {(z, b): keep.tile([P, 2 * H], BF16, name="w_staged_%d_%d" % (z, b), align_bytes=64)[:] for z in range(PASSES) for b in range(2)}
        late_planes = turns.tile([P, 2 * CHUNK], U8, name="late_planes", align_bytes=64, offset=0)

        def quantise_x(z, n0, n1, values):
            nc.vector.quantize_mx(out=x_codes[z][:, n0:n1].bitcast(FP8X4), scales=x_plane(z, n0, n1), in_=values)

        def deal(engine, z, b, m0, m1):
            if engine == "scalar":
                dst = staged[z, b].rearrange("p (t m j) -> p m j t", t=2, j=4)[:, m0:m1]
                src = w_raw[z].rearrange("p j (m t) -> p m j t", t=4)[:, m0:m1, :, 2 * b : 2 * b + 2]
            else:
                dst = staged[z, b].rearrange("p (t g i j) -> p g j i t", t=2, i=2, j=4)[:, m0 // 2 : m1 // 2]
                src = w_raw[z].rearrange("p j (g i t) -> p g j i t", i=2, t=4)[:, m0 // 2 : m1 // 2, :, :, 2 * b : 2 * b + 2]
            cast(engine, dst, src)

        def quantise_w(z, t0, t1):
            cols = slice(t0 * P, t1 * P)
            b = t0 // 2
            values = staged[z, b][:, (t0 - 2 * b) * 4 * P : (t1 - 2 * b) * 4 * P]
            nc.vector.quantize_mx(out=w_codes[z][:, cols].bitcast(FP8X4), scales=w_scales[z][:, cols], in_=values)

        grouped0 = [keep.tile([P, 2 * S], BF16, name="grouped_0_%d" % a, align_bytes=64)[:] for a in range(2)]
        grouped1 = keep.tile([P, 4 * 3 * CHUNK], BF16, name="grouped_1", align_bytes=64)
        grouped_last = turns.tile([P, 4 * CHUNK], BF16, name="grouped_last", align_bytes=64, offset=1024)
        gather("scalar", 0, 0, 0, S)
        gather("vector", 0, 1, 0, S)
        for a in range(2):
            gather("scalar", 0, 2, a * 256, (a + 1) * 256)
            gather("vector", 0, 3, a * 256, (a + 1) * 256)
        interleave("vector", grouped0[0], 0, 0, 256)
        interleave("vector", grouped0[1][:, 0:512], 0, 256, 384)
        interleave("scalar", grouped0[1][:, 512:1024], 0, 384, S)
        for a in range(2):
            quantise_x(0, a * 256, (a + 1) * 256, grouped0[a])
        gather("scalar", 1, 0, 0, S)
        gather("vector", 1, 1, 0, S)
        gather("scalar", 1, 2, 0, CHUNK)
        gather("vector", 1, 2, CHUNK, S)
        for b in range(2):
            deal("scalar", 0, b, 0, 48)
            deal("vector", 0, b, 48, P)
        quantise_w(0, 0, 2)
        quantise_w(0, 2, 4)
        for c in range(CHUNKS):
            gather("scalar", 1, 3, c * CHUNK, (c + 1) * CHUNK)
        interleave("vector", grouped1[:, 0:512], 1, 0, 128)
        interleave("vector", grouped1[:, 512:1024], 1, 128, 256)
        quantise_x(1, 0, CHUNK, grouped1[:, 0:512])
        interleave("vector", grouped1[:, 1024:1536], 1, 256, 384)
        quantise_x(1, CHUNK, 2 * CHUNK, grouped1[:, 512:1024])
        for b, share in enumerate((44, 48)):
            deal("scalar", 1, b, 0, share)
            deal("vector", 1, b, share, P)
        quantise_w(1, 0, 2)
        quantise_w(1, 2, 3)
        quantise_w(1, 3, 4)
        quantise_x(1, 2 * CHUNK, 3 * CHUNK, grouped1[:, 1024:1536])
        interleave("vector", grouped_last[:], 1, 384, S)
        quantise_x(1, 3 * CHUNK, S, grouped_last[:])

        first_bank = psum.tile([P, 512], F32, name="first_bank", tag="first_bank")
        h_banks = [psum.tile([P, 512], F32, name="h_bank_%d" % c) for c in range(CHUNKS)]
        out_banks = {c: psum.tile([P, 512], F32, name="out_bank_%d" % c) for c in range(1, CHUNKS)}

        def hidden_pass(z, c, t):
            cols = slice(c * CHUNK, (c + 1) * CHUNK)
            nc.tensor.matmul_mx(
                out=(first_bank if c == 0 and t < 2 else h_banks[c])[:, t * CHUNK : (t + 1) * CHUNK],
                lhsT=w_codes[z][:, t * P : (t + 1) * P].bitcast(FP8X4),
                lhsT_scale=w_scales[z][:, t * P : (t + 1) * P],
                rhs=x_codes[z][:, cols].bitcast(FP8X4),
                rhs_scale=x_plane(z, cols.start, cols.stop),
                start=(z == 0 and (t == 0 or (c == 0 and t == 2))),
                stop=(z == 1 and (t == 3 or (c == 0 and t == 1))),
            )

        def own_pass(z, c, start, stop):
            cols = slice(c * CHUNK, (c + 1) * CHUNK)
            nc.tensor.matmul_mx(
                out=out_banks[c][:, 0:CHUNK],
                lhsT=w1_sb[:, z * 2 * N : (z + 1) * 2 * N].bitcast(FP4X4),
                lhsT_scale=w4_scales[:, z * N : (z + 1) * N],
                rhs=x_codes[z][:, cols].bitcast(FP8X4),
                rhs_scale=x_plane(z, cols.start, cols.stop),
                start=start,
                stop=stop,
            )

        for ts in ((0, 1), (2, 3)):
            for c in range(CHUNKS):
                for t in ts:
                    hidden_pass(0, c, t)
        for c in range(CHUNKS):
            for t in range(4):
                hidden_pass(1, c, t)
        for c in range(1, CHUNKS):
            own_pass(0, c, True, False)
            own_pass(1, c, False, False)
        for c in range(CHUNKS):
            cols = slice(c * CHUNK, (c + 1) * CHUNK)
            h = keep.tile([P, 4 * CHUNK], BF16, name="h_%d" % c, align_bytes=256)
            if c == 0:
                pairs = keep.tile([P, 4 * CHUNK], BF16, name="pairs", align_bytes=64)
                for b, bank in enumerate((first_bank, h_banks[0])):
                    nc.scalar.activation(
                        pairs[:, b * 2 * CHUNK : (b + 1) * 2 * CHUNK].rearrange("p (n t) -> p n t", t=2),
                        bank[:, b * 2 * CHUNK : (b + 1) * 2 * CHUNK].rearrange("p (t n) -> p n t", t=2),
                        ACT.Gelu_apprx_tanh,
                        bias=bias[:],
                    )
                weave(h[:], pairs[:].bitcast(I32))
                out_banks[0] = psum.tile([P, 512], F32, name="out_bank_0", tag="first_bank")
                own_pass(0, 0, True, False)
                own_pass(1, 0, False, False)
            else:
                nc.scalar.activation(
                    h[:].rearrange("p (n t) -> p n t", t=4),
                    h_banks[c][:].rearrange("p (t n) -> p n t", t=4),
                    ACT.Gelu_apprx_tanh,
                    bias=(zero if c == CHUNKS - 1 else bias)[:],
                )
            h_codes = keep.tile([P, CHUNK], U32, name="h_codes_%d" % c, align_bytes=64)
            h_scales = keep.tile([P, CHUNK], U8, name="h_scales_%d" % c, align_bytes=64)
            nc.vector.quantize_mx(out=h_codes[:].bitcast(FP8X4), scales=h_scales[:], in_=h[:])
            nc.tensor.matmul_mx(
                out=out_banks[c][:, 0:CHUNK],
                lhsT=w3_sb[:].bitcast(FP4X4),
                lhsT_scale=w4_scales[:, 2 * N : 3 * N],
                rhs=h_codes[:].bitcast(FP8X4),
                rhs_scale=h_scales[:],
                start=False,
                stop=True,
            )
        early = turns.tile([P, 2 * CHUNK], F32, name="early", align_bytes=256, offset=8192)
        late = turns.tile([P, 2 * CHUNK], F32, name="late", align_bytes=256, offset=9216)
        for c in range(CHUNKS):
            result = (early, late)[c // 2][:, c % 2 * CHUNK : (c % 2 + 1) * CHUNK]
            nc.vector.tensor_copy(out=result, in_=out_banks[c][:, 0:CHUNK])
            if c == 1:
                nc.sync.dma_start(out=out[:, 0 : 2 * CHUNK], in_=early[:])
            if c > 1:
                nc.sync.dma_start(out=out[:, c * CHUNK : (c + 1) * CHUNK], in_=result)
